import numpy as np
import ml_dtypes


def mxq(x, axis, fmt="e4m3"):
    dtype, down = {"e4m3": (ml_dtypes.float8_e4m3fn, 7), "e5m2": (ml_dtypes.float8_e5m2, 14)}[fmt]
    v = np.moveaxis(np.asarray(x, np.float32).astype(ml_dtypes.bfloat16).astype(np.float64), axis, -1)
    blocks = v.reshape(v.shape[:-1] + (-1, 32))
    amax = np.abs(blocks).max(-1, keepdims=True)
    byte = np.maximum(np.where(amax > 0, np.frexp(amax)[1] - 1 + 127, 0) - down, 1)
    scale = np.exp2(byte - 127.0)
    codes = (blocks / scale).astype(np.float32).astype(dtype).astype(np.float64)
    return np.moveaxis((codes * scale).reshape(v.shape), -1, axis)


WIDE = False


def mx_kscale(k):
    if not WIDE:
        return np.ones(k)
    levels = np.array([10, -10, 5, -5, 0])
    if k % 512:
        return np.exp2(np.random.permutation(np.resize(levels, k // 32))).repeat(32)
    a = np.empty((k // 512, 16))
    for p in range(k // 512):
        a[p, :8] = np.random.permutation(np.resize(levels, 8))
        for g in range(8):
            far = levels[np.abs(levels - a[p, g]) >= 10]
            a[p, g + 8] = far[np.random.randint(len(far))]
    return np.exp2(a.ravel()).repeat(32)


def f64(x):
    return np.asarray(x).astype(np.float64)


def striped(idx):
    return np.tile(idx.reshape(-1, 16).T, (8, 1)).astype(np.uint16)


def unstriped(offs):
    return offs[:16].T.reshape(-1).astype(np.int64)


def pack_weight(w):
    k, n = w.shape
    w = f64(np.asarray(w, np.float32).astype(ml_dtypes.bfloat16)).reshape(k // 32, 32, n)
    amax = np.abs(w).max(1)
    byte = np.clip(np.where(amax > 0, np.frexp(amax)[1] - 1 + 127 - 7, 1), 1, 254)
    scaled = (w * np.exp2(127.0 - byte)[:, None, :]).reshape(k, n).astype(np.float32)
    words = np.ascontiguousarray(scaled.reshape(k // 512, 128, 4, n).transpose(0, 1, 3, 2)).astype(ml_dtypes.float8_e4m3fn).view(np.uint8)
    return words, np.ascontiguousarray(byte.astype(np.uint8).reshape(k // 512, 16, n))


def unpack_weight(words, scales):
    g, p, n, _ = words.shape
    vals = np.ascontiguousarray(words).view(ml_dtypes.float8_e4m3fn).astype(np.float64) * np.repeat(np.exp2(scales.astype(np.float64) - 127.0), 8, axis=1)[..., None]
    return vals.transpose(0, 1, 3, 2).reshape(g * 512, n)


K, T, S, H, N = 512, 2048, 1024, 512, 128
P = 2 ** 7


def setup_inputs():
    n = np.random.standard_normal
    s = mx_kscale(K)[:, None]
    u = mx_kscale(H)
    packed_xT = pack_weight(n((K, T)) * s)
    return {
        "x_words": packed_xT[0],
        "x_scales": packed_xT[1],
        "w1": (n((K, H)) / np.sqrt(K) / s * u).astype(np.float32),
        "w2": (n((H, N)) / np.sqrt(H) / u[:, None]).astype(np.float32),
        "lam": np.tile(np.random.uniform(0.1, 0.9, S), (P, 1)).astype(np.float32),
        "mu": np.tile(np.random.uniform(0.1, 0.9, S), (P, 1)).astype(np.float32),
        "offs": striped(np.random.permutation(T)[:S]),
        "pos1": striped(np.random.permutation(S)),
    }


def reference(x_words, x_scales, w1, w2, lam, mu, offs, pos1):
    xq = unpack_weight(x_words, x_scales)[:, unstriped(offs)]
    h = mxq(f64(w1), 0, "e4m3").T @ xq
    z = h * f64(lam)[:1] + h[:, unstriped(pos1)] * f64(mu)[:1]
    return mxq(f64(w2), 0, "e4m3").T @ mxq(z, 0, "e4m3")

@@ -1,0 +1,186 @@
+from contextlib import ExitStack
+
+import concourse.mybir as mybir
+from concourse.masks import make_identity
+
+K, T, S, H, N = 512, 2048, 1024, 512, 128
+FLOPS = 2 * K * H * S + 2 * H * N * S
+
+F32 = mybir.dt.float32
+BF16 = mybir.dt.bfloat16
+I32 = mybir.dt.int32
+U32 = mybir.dt.uint32
+U16 = mybir.dt.uint16
+U8 = mybir.dt.uint8
+FP8X4 = mybir.dt.float8_e4m3fn_x4
+COPY = mybir.ActivationFunctionType.Copy
+MULT = mybir.AluOpType.mult
+ADD = mybir.AluOpType.add
+
+P = 128
+BLOCKS = S // P
+BANK = 512
+WORD_PIECES = [(0, 512), (512, 256), (768, 256)]
+OUT_PIECES = [(0, 2), (2, 2), (4, 2), (6, 1), (7, 1)]
+
+
+def tile_picked_mixup_none_p_kernel(
+    tc, x_words, x_scales, w1, w2, lam, mu, offs, pos1, out
+):
+    nc = tc.nc
+    with ExitStack() as ctx:
+        keep = ctx.enter_context(tc.tile_pool(name="keep", bufs=1))
+        psum = ctx.enter_context(tc.psum_pool(name="psum", bufs=1))
+
+        def bank_a(shape, name):
+            return psum.tile(shape, F32, name=name, tag="a", bufs=3)
+
+        def bank_b(shape, name):
+            return psum.tile(shape, F32, name=name, tag="b", bufs=5)
+
+        offs_sb = keep.tile([P, S // 16], U16, name="offs_sb")
+        pos_sb = keep.tile([P, S // 16], U16, name="pos_sb")
+        scale_table = keep.tile([P, T], U8, name="scale_table", align_bytes=64)
+        word_table = keep.tile([P, T], I32, name="word_table", align_bytes=64)
+        w1_raw = [keep.tile([P, 4, H // 2], F32, name=f"w1_raw{hf}") for hf in range(2)]
+        w2_raw = keep.tile([P, 4, N], F32, name="w2_raw")
+        share_rows = keep.tile([P, P], F32, name="share_rows")
+        ident = keep.tile([P, P], F32, name="ident")
+
+        nc.vector.memset(scale_table[:].bitcast(I32), 0)
+        nc.gpsimd.memset(share_rows[:], 0.0)
+        make_identity(nc, ident[:])
+
+        w1_rows = w1.rearrange("(p j) c -> p j c", j=4)
+        nc.sync.dma_start(offs_sb[:], offs)
+        nc.sync.dma_start(pos_sb[:], pos1)
+        for q in range(4):
+            nc.sync.dma_start(
+                scale_table[32 * q : 32 * q + 4, :].bitcast(I32),
+                x_scales[0][4 * q : 4 * q + 4, :].bitcast(I32),
+            )
+        nc.sync.dma_start(w1_raw[0][:], w1_rows[:, :, 0 : H // 2])
+        nc.sync.dma_start(word_table[:], x_words[0].rearrange("p n t -> p (n t)").bitcast(I32))
+        nc.sync.dma_start(w1_raw[1][:], w1_rows[:, :, H // 2 : H])
+        nc.sync.dma_start(w2_raw[:], w2.rearrange("(p j) n -> p j n", j=4))
+        for r, share in enumerate((lam, mu)):
+            nc.sync.dma_start(
+                share_rows[BLOCKS * r : BLOCKS * (r + 1), :],
+                share[0:1, :].rearrange("o (b c) -> (o b) c", c=P),
+            )
+
+        x_scale = keep.tile([P, S], U8, name="x_scale", align_bytes=64)
+        x_code = keep.tile([P, S], U32, name="x_code", align_bytes=64)
+        nc.vector.tensor_copy(x_scale[:], scale_table[:].indirect(offs_sb[:]))
+
+        w1_code = [keep.tile([P, 2 * P], U32, name=f"w1_code{hf}", align_bytes=64) for hf in range(2)]
+        w1_scale = [keep.tile([P, 2 * P], U8, name=f"w1_scale{hf}", align_bytes=64) for hf in range(2)]
+
+        def quantise_w1(hf, on_scalar):
+            grouped = keep.tile([P, 2 * P * 4], BF16, name=f"w1_grouped{hf}", align_bytes=64)
+            dst = grouped[:].rearrange("p (u q e j) -> p q u e j", u=2, e=2, j=4)
+            src = w1_raw[hf][:].rearrange("p j (q u e) -> p q u e j", u=2, e=2)
+            if on_scalar:
+                nc.scalar.activation(dst, src, COPY)
+            else:
+                nc.vector.tensor_copy(dst, src)
+            nc.vector.quantize_mx(w1_code[hf][:].bitcast(FP8X4), w1_scale[hf][:], grouped[:])
+
+        quantise_w1(0, True)
+        for t0, n in WORD_PIECES:
+            nc.vector.tensor_copy(
+                x_code[:, t0 : t0 + n],
+                word_table[:].bitcast(U32).indirect(offs_sb[:, t0 // 16 : (t0 + n) // 16]),
+            )
+        quantise_w1(1, False)
+
+        h = [keep.tile([P, S], F32, name=f"h{c}") for c in range(4)]
+
+        def first_product(c, t0, n):
+            u, hf = divmod(c, 2)
+            acc = bank_a([P, n], f"h_acc{c}_{t0}")
+            nc.tensor.matmul_mx(
+                acc[:],
+                lhsT=w1_code[hf][:, u * P : (u + 1) * P].bitcast(FP8X4),
+                lhsT_scale=w1_scale[hf][:, u * P : (u + 1) * P],
+                rhs=x_code[:, t0 : t0 + n].bitcast(FP8X4),
+                rhs_scale=x_scale[:, t0 : t0 + n],
+                start=True,
+                stop=True,
+            )
+            nc.scalar.copy(h[c][:, t0 : t0 + n], acc[:])
+
+        first_product(0, 0, 512)
+        first_product(2, 0, 512)
+        first_product(0, 512, 256)
+        first_product(0, 768, 256)
+        first_product(2, 512, 512)
+        for c in (1, 3):
+            for t0 in (0, 512):
+                first_product(c, t0, 512)
+
+        w2_grouped = keep.tile([P, N * 4], BF16, name="w2_grouped", align_bytes=64)
+        w2_code = keep.tile([P, N], U32, name="w2_code", align_bytes=64)
+        w2_scale = keep.tile([P, N], U8, name="w2_scale", align_bytes=64)
+        nc.vector.tensor_copy(
+            w2_grouped[:].rearrange("p (n j) -> p n j", j=4), w2_raw[:].rearrange("p j n -> p n j")
+        )
+        nc.vector.quantize_mx(w2_code[:].bitcast(FP8X4), w2_scale[:], w2_grouped[:])
+
+        shares = keep.tile([P, 2 * BLOCKS], F32, name="shares")
+        shares_t = bank_b([P, P], "shares_t")
+        nc.tensor.transpose(shares_t[:], share_rows[:], ident[:])
+        nc.scalar.copy(shares[:], shares_t[:, 0 : 2 * BLOCKS])
+
+        partner = {}
+        for r in range(2):
+            for c in (0, 2, 1, 3):
+                partner[c, r] = keep.tile([P, 512], F32, name=f"partner{c}_{r}")
+                nc.vector.tensor_copy(partner[c, r][:], h[c][:].indirect(pos_sb[:, 32 * r : 32 * (r + 1)]))
+
+        own = []
+        for b in range(BLOCKS):
+            h_t = bank_b([P, H], f"h_t{b}")
+            for c in range(4):
+                nc.tensor.transpose(h_t[:, c * P : (c + 1) * P], h[c][:, b * P : (b + 1) * P], ident[:])
+            own.append(keep.tile([P, H], F32, name=f"own{b}"))
+            nc.scalar.activation(own[b][:], h_t[:], COPY, scale=shares[:, b : b + 1])
+
+        for b0, nb in OUT_PIECES:
+            n = nb * P
+            pairs = bank_a([P, nb, 2, P], f"pairs{b0}")
+            for i in range(nb):
+                b = b0 + i
+                r, col = divmod(b * P, 512)
+                partner_t = bank_b([P, H], f"partner_t{b}")
+                for c in range(4):
+                    nc.tensor.transpose(
+                        partner_t[:, c * P : (c + 1) * P], partner[c, r][:, col : col + P], ident[:]
+                    )
+                z_t = keep.tile([P, H], BF16, name=f"z_t{b}")
+                nc.vector.scalar_tensor_tensor(
+                    z_t[:], partner_t[:], shares[:, BLOCKS + b : BLOCKS + b + 1], own[b][:], MULT, ADD
+                )
+                for u in range(2):
+                    nc.tensor.transpose(pairs[:, i, u, :], z_t[:].bitcast(F32)[:, u * P : (u + 1) * P], ident[:])
+            z = keep.tile([P, 4 * n], BF16, name=f"z{b0}", align_bytes=64)
+            nc.scalar.copy(
+                z[:].bitcast(F32).rearrange("p (i n u) -> p i n u", i=nb, u=2),
+                pairs[:].rearrange("p i u n -> p i n u"),
+            )
+            z_code = keep.tile([P, n], U32, name=f"z_code{b0}", align_bytes=64)
+            z_scale = keep.tile([P, n], U8, name=f"z_scale{b0}", align_bytes=64)
+            nc.vector.quantize_mx(z_code[:].bitcast(FP8X4), z_scale[:], z[:])
+            acc = bank_a([P, n], f"out_acc{b0}")
+            nc.tensor.matmul_mx(
+                acc[:],
+                lhsT=w2_code[:].bitcast(FP8X4),
+                lhsT_scale=w2_scale[:],
+                rhs=z_code[:].bitcast(FP8X4),
+                rhs_scale=z_scale[:],
+                start=True,
+                stop=True,
+            )
+            res = keep.tile([P, n], F32, name=f"res{b0}")
+            nc.scalar.copy(res[:], acc[:])
+            nc.sync.dma_start(out[:, b0 * P : b0 * P + n], res[:])

@@ -21,7 +21,8 @@ P = 128
 BLOCKS = S // P
 BANK = 512
 WORD_PIECES = [(0, 512), (512, 256), (768, 256)]
-OUT_PIECES = [(0, 2), (2, 2), (4, 2), (6, 1), (7, 1)]
+GROUPS = [(0, 2), (2, 2), (4, 2), (6, 1), (7, 1)]
+ROUNDS = [(0, 512), (512, 256), (768, 256)]
 
 
 def tile_picked_mixup_none_p_kernel(
@@ -31,19 +32,13 @@ def tile_picked_mixup_none_p_kernel(
     with ExitStack() as ctx:
         keep = ctx.enter_context(tc.tile_pool(name="keep", bufs=1))
         psum = ctx.enter_context(tc.psum_pool(name="psum", bufs=1))
-
-        def bank_a(shape, name):
-            return psum.tile(shape, F32, name=name, tag="a", bufs=3)
-
-        def bank_b(shape, name):
-            return psum.tile(shape, F32, name=name, tag="b", bufs=5)
+        banks = [psum.tile([P, BANK], F32, name=f"bank{i}") for i in range(8)]
 
         offs_sb = keep.tile([P, S // 16], U16, name="offs_sb")
         pos_sb = keep.tile([P, S // 16], U16, name="pos_sb")
         scale_table = keep.tile([P, T], U8, name="scale_table", align_bytes=64)
         word_table = keep.tile([P, T], I32, name="word_table", align_bytes=64)
-        w1_raw = [keep.tile([P, 4, H // 2], F32, name=f"w1_raw{hf}") for hf in range(2)]
-        w2_raw = keep.tile([P, 4, N], F32, name="w2_raw")
+        w1_raw = [keep.tile([P, 4, H // 2], F32, name=f"w1_raw{hf}", tag=f"raw{hf}") for hf in range(2)]
         share_rows = keep.tile([P, P], F32, name="share_rows")
         ident = keep.tile([P, P], F32, name="ident")
 
@@ -62,7 +57,6 @@ def tile_picked_mixup_none_p_kernel(
         nc.sync.dma_start(w1_raw[0][:], w1_rows[:, :, 0 : H // 2])
         nc.sync.dma_start(word_table[:], x_words[0].rearrange("p n t -> p (n t)").bitcast(I32))
         nc.sync.dma_start(w1_raw[1][:], w1_rows[:, :, H // 2 : H])
-        nc.sync.dma_start(w2_raw[:], w2.rearrange("(p j) n -> p j n", j=4))
         for r, share in enumerate((lam, mu)):
             nc.sync.dma_start(
                 share_rows[BLOCKS * r : BLOCKS * (r + 1), :],
@@ -70,37 +64,39 @@ def tile_picked_mixup_none_p_kernel(
             )
 
         x_scale = keep.tile([P, S], U8, name="x_scale", align_bytes=64)
-        x_code = keep.tile([P, S], U32, name="x_code", align_bytes=64)
         nc.vector.tensor_copy(x_scale[:], scale_table[:].indirect(offs_sb[:]))
 
         w1_code = [keep.tile([P, 2 * P], U32, name=f"w1_code{hf}", align_bytes=64) for hf in range(2)]
         w1_scale = [keep.tile([P, 2 * P], U8, name=f"w1_scale{hf}", align_bytes=64) for hf in range(2)]
 
-        def quantise_w1(hf, on_scalar):
-            grouped = keep.tile([P, 2 * P * 4], BF16, name=f"w1_grouped{hf}", align_bytes=64)
-            dst = grouped[:].rearrange("p (u q e j) -> p q u e j", u=2, e=2, j=4)
-            src = w1_raw[hf][:].rearrange("p j (q u e) -> p q u e j", u=2, e=2)
-            if on_scalar:
-                nc.scalar.activation(dst, src, COPY)
-            else:
-                nc.vector.tensor_copy(dst, src)
+        def quantise_w1(hf):
+            grouped = keep.tile([P, 2 * P * 4], BF16, name=f"w1_grouped{hf}", tag=f"grouped{hf}", align_bytes=64)
+            nc.scalar.activation(
+                grouped[:].rearrange("p (u q e j) -> p q u e j", u=2, e=2, j=4),
+                w1_raw[hf][:].rearrange("p j (q u e) -> p q u e j", u=2, e=2),
+                COPY,
+            )
             nc.vector.quantize_mx(w1_code[hf][:].bitcast(FP8X4), w1_scale[hf][:], grouped[:])
 
-        quantise_w1(0, True)
+        quantise_w1(0)
+        x_code = keep.tile([P, S], U32, name="x_code", tag="grouped0", align_bytes=64)
         for t0, n in WORD_PIECES:
             nc.vector.tensor_copy(
                 x_code[:, t0 : t0 + n],
                 word_table[:].bitcast(U32).indirect(offs_sb[:, t0 // 16 : (t0 + n) // 16]),
             )
-        quantise_w1(1, False)
+        quantise_w1(1)
+        w2_raw = keep.tile([P, 4, N], F32, name="w2_raw", tag="raw1")
+        nc.sync.dma_start(w2_raw[:], w2.rearrange("(p j) n -> p j n", j=4))
 
         h = [keep.tile([P, S], F32, name=f"h{c}") for c in range(4)]
-
-        def first_product(c, t0, n):
+        passes = [(0, 0, 512), (2, 0, 512), (0, 512, 256), (0, 768, 256), (2, 512, 512)]
+        passes = passes + [(c, t0, 512) for c in (1, 3) for t0 in (0, 512)]
+        for i, (c, t0, n) in enumerate(passes):
             u, hf = divmod(c, 2)
-            acc = bank_a([P, n], f"h_acc{c}_{t0}")
+            acc = banks[i % 7][:, 0:n]
             nc.tensor.matmul_mx(
-                acc[:],
+                acc,
                 lhsT=w1_code[hf][:, u * P : (u + 1) * P].bitcast(FP8X4),
                 lhsT_scale=w1_scale[hf][:, u * P : (u + 1) * P],
                 rhs=x_code[:, t0 : t0 + n].bitcast(FP8X4),
@@ -108,72 +104,69 @@ def tile_picked_mixup_none_p_kernel(
                 start=True,
                 stop=True,
             )
-            nc.scalar.copy(h[c][:, t0 : t0 + n], acc[:])
-
-        first_product(0, 0, 512)
-        first_product(2, 0, 512)
-        first_product(0, 512, 256)
-        first_product(0, 768, 256)
-        first_product(2, 512, 512)
-        for c in (1, 3):
-            for t0 in (0, 512):
-                first_product(c, t0, 512)
-
-        w2_grouped = keep.tile([P, N * 4], BF16, name="w2_grouped", align_bytes=64)
-        w2_code = keep.tile([P, N], U32, name="w2_code", align_bytes=64)
-        w2_scale = keep.tile([P, N], U8, name="w2_scale", align_bytes=64)
-        nc.vector.tensor_copy(
-            w2_grouped[:].rearrange("p (n j) -> p n j", j=4), w2_raw[:].rearrange("p j n -> p n j")
-        )
-        nc.vector.quantize_mx(w2_code[:].bitcast(FP8X4), w2_scale[:], w2_grouped[:])
+            if (c, t0) == (2, 0):
+                nc.vector.tensor_copy(h[c][:, t0 : t0 + n], acc)
+            else:
+                nc.scalar.copy(h[c][:, t0 : t0 + n], acc)
 
         shares = keep.tile([P, 2 * BLOCKS], F32, name="shares")
-        shares_t = bank_b([P, P], "shares_t")
-        nc.tensor.transpose(shares_t[:], share_rows[:], ident[:])
-        nc.scalar.copy(shares[:], shares_t[:, 0 : 2 * BLOCKS])
+        nc.tensor.transpose(banks[7][:, 0:P], share_rows[:], ident[:])
+        nc.scalar.copy(shares[:], banks[7][:, 0 : 2 * BLOCKS])
 
         partner = {}
-        for r in range(2):
+        for t0, n in ROUNDS:
             for c in (0, 2, 1, 3):
-                partner[c, r] = keep.tile([P, 512], F32, name=f"partner{c}_{r}")
-                nc.vector.tensor_copy(partner[c, r][:], h[c][:].indirect(pos_sb[:, 32 * r : 32 * (r + 1)]))
+                piece = keep.tile([P, n], F32, name=f"partner{c}_{t0}")
+                nc.vector.tensor_copy(piece[:], h[c][:].indirect(pos_sb[:, t0 // 16 : (t0 + n) // 16]))
+                for i in range(n // P):
+                    partner[c, t0 // P + i] = piece[:, i * P : (i + 1) * P]
 
         own = []
         for b in range(BLOCKS):
-            h_t = bank_b([P, H], f"h_t{b}")
+            h_t = banks[2 + b % 6]
             for c in range(4):
                 nc.tensor.transpose(h_t[:, c * P : (c + 1) * P], h[c][:, b * P : (b + 1) * P], ident[:])
             own.append(keep.tile([P, H], F32, name=f"own{b}"))
             nc.scalar.activation(own[b][:], h_t[:], COPY, scale=shares[:, b : b + 1])
 
-        for b0, nb in OUT_PIECES:
-            n = nb * P
-            pairs = bank_a([P, nb, 2, P], f"pairs{b0}")
-            for i in range(nb):
-                b = b0 + i
-                r, col = divmod(b * P, 512)
-                partner_t = bank_b([P, H], f"partner_t{b}")
-                for c in range(4):
-                    nc.tensor.transpose(
-                        partner_t[:, c * P : (c + 1) * P], partner[c, r][:, col : col + P], ident[:]
-                    )
-                z_t = keep.tile([P, H], BF16, name=f"z_t{b}")
-                nc.vector.scalar_tensor_tensor(
-                    z_t[:], partner_t[:], shares[:, BLOCKS + b : BLOCKS + b + 1], own[b][:], MULT, ADD
-                )
-                for u in range(2):
-                    nc.tensor.transpose(pairs[:, i, u, :], z_t[:].bitcast(F32)[:, u * P : (u + 1) * P], ident[:])
-            z = keep.tile([P, 4 * n], BF16, name=f"z{b0}", align_bytes=64)
-            nc.scalar.copy(
-                z[:].bitcast(F32).rearrange("p (i n u) -> p i n u", i=nb, u=2),
-                pairs[:].rearrange("p i u n -> p i n u"),
+        w2_grouped = keep.tile([P, N * 4], BF16, name="w2_grouped", align_bytes=64)
+        w2_code = keep.tile([P, N], U32, name="w2_code", align_bytes=64)
+        w2_scale = keep.tile([P, N], U8, name="w2_scale", align_bytes=64)
+        nc.scalar.copy(w2_grouped[:].rearrange("p (n j) -> p n j", j=4), w2_raw[:].rearrange("p j n -> p n j"))
+        nc.vector.quantize_mx(w2_code[:].bitcast(FP8X4), w2_scale[:], w2_grouped[:])
+
+        z_t = []
+        for b in range(BLOCKS):
+            partner_t = banks[2 + (BLOCKS + b) % 6]
+            for c in range(4):
+                nc.tensor.transpose(partner_t[:, c * P : (c + 1) * P], partner[c, b], ident[:])
+            z_t.append(keep.tile([P, H], BF16, name=f"z_t{b}"))
+            nc.vector.scalar_tensor_tensor(
+                z_t[b][:], partner_t[:], shares[:, BLOCKS + b : BLOCKS + b + 1], own[b][:], MULT, ADD
             )
-            z_code = keep.tile([P, n], U32, name=f"z_code{b0}", align_bytes=64)
-            z_scale = keep.tile([P, n], U8, name=f"z_scale{b0}", align_bytes=64)
-            nc.vector.quantize_mx(z_code[:].bitcast(FP8X4), z_scale[:], z[:])
-            acc = bank_a([P, n], f"out_acc{b0}")
+
+        z = []
+        for g, (b0, nb) in enumerate(GROUPS):
+            pairs = banks[g % 2][:, 0 : nb * 2 * P].rearrange("p (i u n) -> p i u n", i=nb, u=2)
+            for i in range(nb):
+                for u in range(2):
+                    nc.tensor.transpose(
+                        pairs[:, i, u, :], z_t[b0 + i][:].bitcast(F32)[:, u * P : (u + 1) * P], ident[:]
+                    )
+            z.append(keep.tile([P, 4 * nb * P], BF16, name=f"z{g}", align_bytes=64))
+            nc.scalar.copy(
+                z[g][:].bitcast(F32).rearrange("p (i n u) -> p i n u", i=nb, u=2),
+                pairs.rearrange("p i u n -> p i n u"),
+            )
+
+        for g, (b0, nb) in enumerate(GROUPS):
+            n = nb * P
+            z_code = keep.tile([P, n], U32, name=f"z_code{g}", align_bytes=64)
+            z_scale = keep.tile([P, n], U8, name=f"z_scale{g}", align_bytes=64)
+            nc.vector.quantize_mx(z_code[:].bitcast(FP8X4), z_scale[:], z[g][:])
+            acc = banks[[6, 7, 2, 3, 4][g]][:, 0:n]
             nc.tensor.matmul_mx(
-                acc[:],
+                acc,
                 lhsT=w2_code[:].bitcast(FP8X4),
                 lhsT_scale=w2_scale[:],
                 rhs=z_code[:].bitcast(FP8X4),
@@ -181,6 +174,9 @@ def tile_picked_mixup_none_p_kernel(
                 start=True,
                 stop=True,
             )
-            res = keep.tile([P, n], F32, name=f"res{b0}")
-            nc.scalar.copy(res[:], acc[:])
+            res = keep.tile([P, n], F32, name=f"res{g}")
+            if g < 3:
+                nc.scalar.copy(res[:], acc)
+            else:
+                nc.vector.tensor_copy(res[:], acc)
             nc.sync.dma_start(out[:, b0 * P : b0 * P + n], res[:])

@@ -20,9 +20,11 @@ ADD = mybir.AluOpType.add
 P = 128
 BLOCKS = S // P
 BANK = 512
-WORD_PIECES = [(0, 512), (512, 256), (768, 256)]
-GROUPS = [(0, 2), (2, 2), (4, 2), (6, 1), (7, 1)]
-ROUNDS = [(0, 512), (512, 256), (768, 256)]
+TILES = H // P
+FIRST_PASSES = [(t0, 256) for t0 in range(0, S, 256)]
+DIRECT_BLOCKS = 2
+GROUPS = [(0, 2), (2, 2), (4, 2), (6, 2)]
+POOL_BLOCKS = 8
 
 
 def tile_picked_mixup_none_p_kernel(
@@ -31,119 +33,170 @@ def tile_picked_mixup_none_p_kernel(
     nc = tc.nc
     with ExitStack() as ctx:
         keep = ctx.enter_context(tc.tile_pool(name="keep", bufs=1))
+        shared = ctx.enter_context(tc.tile_pool(name="shared", bufs=1))
         psum = ctx.enter_context(tc.psum_pool(name="psum", bufs=1))
         banks = [psum.tile([P, BANK], F32, name=f"bank{i}") for i in range(8)]
 
         offs_sb = keep.tile([P, S // 16], U16, name="offs_sb")
         pos_sb = keep.tile([P, S // 16], U16, name="pos_sb")
         scale_table = keep.tile([P, T], U8, name="scale_table", align_bytes=64)
-        word_table = keep.tile([P, T], I32, name="word_table", align_bytes=64)
-        w1_raw = [keep.tile([P, 4, H // 2], F32, name=f"w1_raw{hf}", tag=f"raw{hf}") for hf in range(2)]
+        word_table = shared.tile([P, T], I32, name="word_table", align_bytes=64, offset=0)
+        w1_raw = [keep.tile([P, 4, P], F32, name=f"w1_raw{t}", tag=f"raw{t}") for t in range(TILES)]
         share_rows = keep.tile([P, P], F32, name="share_rows")
         ident = keep.tile([P, P], F32, name="ident")
 
-        nc.vector.memset(scale_table[:].bitcast(I32), 0)
+        nc.vector.memset(scale_table[:, 0 : T // 2].bitcast(I32), 0)
         nc.gpsimd.memset(share_rows[:], 0.0)
+        nc.gpsimd.memset(scale_table[:, T // 2 : T].bitcast(I32), 0)
         make_identity(nc, ident[:])
 
         w1_rows = w1.rearrange("(p j) c -> p j c", j=4)
         nc.sync.dma_start(offs_sb[:], offs)
-        nc.sync.dma_start(pos_sb[:], pos1)
-        for q in range(4):
-            nc.sync.dma_start(
-                scale_table[32 * q : 32 * q + 4, :].bitcast(I32),
-                x_scales[0][4 * q : 4 * q + 4, :].bitcast(I32),
-            )
-        nc.sync.dma_start(w1_raw[0][:], w1_rows[:, :, 0 : H // 2])
-        nc.sync.dma_start(word_table[:], x_words[0].rearrange("p n t -> p (n t)").bitcast(I32))
-        nc.sync.dma_start(w1_raw[1][:], w1_rows[:, :, H // 2 : H])
         for r, share in enumerate((lam, mu)):
             nc.sync.dma_start(
                 share_rows[BLOCKS * r : BLOCKS * (r + 1), :],
                 share[0:1, :].rearrange("o (b c) -> (o b) c", c=P),
             )
+        for q in range(4):
+            nc.sync.dma_start(
+                scale_table[32 * q : 32 * q + 4, :].bitcast(I32),
+                x_scales[0][4 * q : 4 * q + 4, :].bitcast(I32),
+            )
+        nc.sync.dma_start(w1_raw[0][:], w1_rows[:, :, 0:P])
+        nc.sync.dma_start(word_table[:], x_words[0].rearrange("p n t -> p (n t)").bitcast(I32))
+        for t in range(1, TILES):
+            nc.sync.dma_start(w1_raw[t][:], w1_rows[:, :, t * P : (t + 1) * P])
+        nc.sync.dma_start(pos_sb[:], pos1)
+
+        shares = keep.tile([P, 2 * BLOCKS], F32, name="shares")
+        nc.tensor.transpose(banks[7][:, 0:P], share_rows[:], ident[:])
+        nc.scalar.activation(shares[:], banks[7][:, 0 : 2 * BLOCKS], COPY)
+
+        w1_code = {}
+        w1_scale = [keep.tile([P, P], U8, name=f"w1_scale{t}", align_bytes=64) for t in range(TILES)]
+
+        def quantise_w1(t, copy):
+            if t == 0:
+                w1_code[t] = keep.tile([P, P], U32, name=f"w1_code{t}", align_bytes=64)
+            else:
+                w1_code[t] = shared.tile([P, P], U32, name=f"w1_code{t}", align_bytes=64, offset=512 * t)
+            grouped = keep.tile([P, P * 4], BF16, name=f"w1_grouped{t}", align_bytes=64)
+            copy(
+                grouped[:].rearrange("p (u q e j) -> p q u e j", u=2, e=2, j=4),
+                w1_raw[t][:].rearrange("p j (q u e) -> p q u e j", u=2, e=2),
+            )
+            nc.vector.quantize_mx(w1_code[t][:].bitcast(FP8X4), w1_scale[t][:], grouped[:])
+
+        def scalar_copy(dst, src):
+            nc.scalar.activation(dst, src, COPY)
+
+        def gather_words(dst, t0, n):
+            nc.vector.tensor_copy(dst, word_table[:].bitcast(U32).indirect(offs_sb[:, t0 // 16 : (t0 + n) // 16]))
 
         x_scale = keep.tile([P, S], U8, name="x_scale", align_bytes=64)
         nc.vector.tensor_copy(x_scale[:], scale_table[:].indirect(offs_sb[:]))
-
-        w1_code = [keep.tile([P, 2 * P], U32, name=f"w1_code{hf}", align_bytes=64) for hf in range(2)]
-        w1_scale = [keep.tile([P, 2 * P], U8, name=f"w1_scale{hf}", align_bytes=64) for hf in range(2)]
-
-        def quantise_w1(hf):
-            grouped = keep.tile([P, 2 * P * 4], BF16, name=f"w1_grouped{hf}", tag=f"grouped{hf}", align_bytes=64)
-            nc.scalar.activation(
-                grouped[:].rearrange("p (u q e j) -> p q u e j", u=2, e=2, j=4),
-                w1_raw[hf][:].rearrange("p j (q u e) -> p q u e j", u=2, e=2),
-                COPY,
-            )
-            nc.vector.quantize_mx(w1_code[hf][:].bitcast(FP8X4), w1_scale[hf][:], grouped[:])
-
-        quantise_w1(0)
-        x_code = keep.tile([P, S], U32, name="x_code", tag="grouped0", align_bytes=64)
-        for t0, n in WORD_PIECES:
-            nc.vector.tensor_copy(
-                x_code[:, t0 : t0 + n],
-                word_table[:].bitcast(U32).indirect(offs_sb[:, t0 // 16 : (t0 + n) // 16]),
-            )
-        quantise_w1(1)
-        w2_raw = keep.tile([P, 4, N], F32, name="w2_raw", tag="raw1")
+        quantise_w1(0, scalar_copy)
+        x_code = keep.tile([P, S], U32, name="x_code", align_bytes=64)
+        for t0, n in FIRST_PASSES:
+            gather_words(x_code[:, t0 : t0 + n], t0, n)
+        quantise_w1(1, scalar_copy)
+        quantise_w1(2, scalar_copy)
+        quantise_w1(3, nc.gpsimd.tensor_copy)
+        w2_raw = keep.tile([P, 4, N], F32, name="w2_raw", tag="raw3")
         nc.sync.dma_start(w2_raw[:], w2.rearrange("(p j) n -> p j n", j=4))
 
-        h = [keep.tile([P, S], F32, name=f"h{c}") for c in range(4)]
-        passes = [(0, 0, 512), (2, 0, 512), (0, 512, 256), (0, 768, 256), (2, 512, 512)]
-        passes = passes + [(c, t0, 512) for c in (1, 3) for t0 in (0, 512)]
-        for i, (c, t0, n) in enumerate(passes):
-            u, hf = divmod(c, 2)
-            acc = banks[i % 7][:, 0:n]
+        h = [keep.tile([P, S], F32, name=f"h{t}") for t in range(TILES)]
+        passes = [(0, t0, n) for t0, n in FIRST_PASSES] + [(t, t0, BANK) for t in range(1, TILES) for t0 in (0, BANK)]
+        for i, (t, t0, n) in enumerate(passes):
+            acc = banks[i % 8][:, 0:n]
             nc.tensor.matmul_mx(
                 acc,
-                lhsT=w1_code[hf][:, u * P : (u + 1) * P].bitcast(FP8X4),
-                lhsT_scale=w1_scale[hf][:, u * P : (u + 1) * P],
+                lhsT=w1_code[t][:].bitcast(FP8X4),
+                lhsT_scale=w1_scale[t][:],
                 rhs=x_code[:, t0 : t0 + n].bitcast(FP8X4),
                 rhs_scale=x_scale[:, t0 : t0 + n],
                 start=True,
                 stop=True,
             )
-            if (c, t0) == (2, 0):
-                nc.vector.tensor_copy(h[c][:, t0 : t0 + n], acc)
-            else:
-                nc.scalar.copy(h[c][:, t0 : t0 + n], acc)
-
-        shares = keep.tile([P, 2 * BLOCKS], F32, name="shares")
-        nc.tensor.transpose(banks[7][:, 0:P], share_rows[:], ident[:])
-        nc.scalar.copy(shares[:], banks[7][:, 0 : 2 * BLOCKS])
+            nc.scalar.copy(h[t][:, t0 : t0 + n], acc)
 
         partner = {}
-        for t0, n in ROUNDS:
-            for c in (0, 2, 1, 3):
-                piece = keep.tile([P, n], F32, name=f"partner{c}_{t0}")
-                nc.vector.tensor_copy(piece[:], h[c][:].indirect(pos_sb[:, t0 // 16 : (t0 + n) // 16]))
+        for t in range(TILES):
+            n = 256 if t == TILES - 1 else 512
+            for t0 in range(0, S, n):
+                piece = keep.tile([P, n], F32, name=f"partner{t}_{t0}")
+                nc.vector.tensor_copy(piece[:], h[t][:].indirect(pos_sb[:, t0 // 16 : (t0 + n) // 16]))
                 for i in range(n // P):
-                    partner[c, t0 // P + i] = piece[:, i * P : (i + 1) * P]
-
-        own = []
-        for b in range(BLOCKS):
-            h_t = banks[2 + b % 6]
-            for c in range(4):
-                nc.tensor.transpose(h_t[:, c * P : (c + 1) * P], h[c][:, b * P : (b + 1) * P], ident[:])
-            own.append(keep.tile([P, H], F32, name=f"own{b}"))
-            nc.scalar.activation(own[b][:], h_t[:], COPY, scale=shares[:, b : b + 1])
+                    partner[t, t0 // P + i] = piece[:, i * P : (i + 1) * P]
 
         w2_grouped = keep.tile([P, N * 4], BF16, name="w2_grouped", align_bytes=64)
         w2_code = keep.tile([P, N], U32, name="w2_code", align_bytes=64)
         w2_scale = keep.tile([P, N], U8, name="w2_scale", align_bytes=64)
-        nc.scalar.copy(w2_grouped[:].rearrange("p (n j) -> p n j", j=4), w2_raw[:].rearrange("p j n -> p n j"))
+        nc.gpsimd.tensor_copy(w2_grouped[:].rearrange("p (n j) -> p n j", j=4), w2_raw[:].rearrange("p j n -> p n j"))
         nc.vector.quantize_mx(w2_code[:].bitcast(FP8X4), w2_scale[:], w2_grouped[:])
 
-        z_t = []
+        turns = []
+
+        def next_bank():
+            turns.append(banks[2 + len(turns) % 6])
+            return turns[-1]
+
+        def by_half(block):
+            return block.rearrange("p (u half m) -> p half u m", u=2, half=2)
+
+        def turn(dst, tiles, sources):
+            by_tile = dst.rearrange("p (u t m) -> p t u m", u=2, t=len(tiles))
+            for i, t in enumerate(tiles):
+                nc.tensor.transpose(by_tile[:, i], sources[t], ident[:])
+
+        own = []
+        z_t = [keep.tile([P, H], BF16, name=f"z_t{b}") for b in range(BLOCKS)]
+        mu_of = [shares[:, BLOCKS + b : BLOCKS + b + 1] for b in range(BLOCKS)]
         for b in range(BLOCKS):
-            partner_t = banks[2 + (BLOCKS + b) % 6]
-            for c in range(4):
-                nc.tensor.transpose(partner_t[:, c * P : (c + 1) * P], partner[c, b], ident[:])
-            z_t.append(keep.tile([P, H], BF16, name=f"z_t{b}"))
-            nc.vector.scalar_tensor_tensor(
-                z_t[b][:], partner_t[:], shares[:, BLOCKS + b : BLOCKS + b + 1], own[b][:], MULT, ADD
+            h_t = next_bank()
+            own.append(keep.tile([P, H], F32, name=f"own{b}"))
+            if b < DIRECT_BLOCKS:
+                for t in range(TILES):
+                    nc.tensor.matmul_mx(
+                        h_t[:, t * P : (t + 1) * P],
+                        lhsT=x_code[:, b * P : (b + 1) * P].bitcast(FP8X4),
+                        lhsT_scale=x_scale[:, b * P : (b + 1) * P],
+                        rhs=w1_code[t][:].bitcast(FP8X4),
+                        rhs_scale=w1_scale[t][:],
+                        start=True,
+                        stop=True,
+                    )
+                rows = h_t[:].rearrange("p (t u m) -> p u t m", t=TILES, u=2)
+            else:
+                turn(h_t[:], range(TILES), [h[t][:, b * P : (b + 1) * P] for t in range(TILES)])
+                rows = h_t[:].rearrange("p (u t m) -> p u t m", t=TILES, u=2)
+            nc.scalar.activation(
+                own[b][:].rearrange("p (u t m) -> p u t m", t=TILES, u=2), rows, COPY, scale=shares[:, b : b + 1]
             )
+            if b < POOL_BLOCKS:
+                low_t = next_bank()[:, 0 : H // 2]
+                turn(low_t, (0, 1), [partner[t, b] for t in range(TILES)])
+                other = keep.tile([P, 2, P], F32, name=f"other{b}")
+                nc.scalar.activation(other[:], low_t.rearrange("p (u m) -> p u m", u=2), COPY, scale=mu_of[b])
+                nc.gpsimd.tensor_tensor(by_half(z_t[b][:])[:, 0], other[:], by_half(own[b][:])[:, 0], ADD)
+        for b0 in range(0, POOL_BLOCKS, 2):
+            bank = next_bank()
+            for i in range(2):
+                turn(bank[:, i * 256 : (i + 1) * 256], (2, 3), [partner[t, b0 + i] for t in range(TILES)])
+            for i in range(2):
+                b = b0 + i
+                nc.vector.scalar_tensor_tensor(
+                    by_half(z_t[b][:])[:, 1],
+                    bank[:, i * 256 : (i + 1) * 256].rearrange("p (u m) -> p u m", u=2),
+                    mu_of[b],
+                    by_half(own[b][:])[:, 1],
+                    MULT,
+                    ADD,
+                )
+        for b in range(POOL_BLOCKS, BLOCKS):
+            partner_t = next_bank()
+            turn(partner_t[:], range(TILES), [partner[t, b] for t in range(TILES)])
+            nc.vector.scalar_tensor_tensor(z_t[b][:], partner_t[:], mu_of[b], own[b][:], MULT, ADD)
 
         z = []
         for g, (b0, nb) in enumerate(GROUPS):
@@ -164,7 +217,7 @@ def tile_picked_mixup_none_p_kernel(
             z_code = keep.tile([P, n], U32, name=f"z_code{g}", align_bytes=64)
             z_scale = keep.tile([P, n], U8, name=f"z_scale{g}", align_bytes=64)
             nc.vector.quantize_mx(z_code[:].bitcast(FP8X4), z_scale[:], z[g][:])
-            acc = banks[[6, 7, 2, 3, 4][g]][:, 0:n]
+            acc = banks[[4, 5, 6, 7][g]][:, 0:n]
             nc.tensor.matmul_mx(
                 acc,
                 lhsT=w2_code[:].bitcast(FP8X4),

@@ -23,7 +23,7 @@ BANK = 512
 TILES = H // P
 FIRST_PASSES = [(t0, 256) for t0 in range(0, S, 256)]
 DIRECT_BLOCKS = 2
-GROUPS = [(0, 2), (2, 2), (4, 2), (6, 2)]
+GROUPS = [(0, 2), (2, 2), (4, 2), (6, 1), (7, 1)]
 POOL_BLOCKS = 8
 
 
@@ -90,6 +90,9 @@ def tile_picked_mixup_none_p_kernel(
         def scalar_copy(dst, src):
             nc.scalar.activation(dst, src, COPY)
 
+        def pool_copy(dst, src):
+            nc.gpsimd.tensor_scalar(dst, src, 1.0, 0.0, MULT, ADD)
+
         def gather_words(dst, t0, n):
             nc.vector.tensor_copy(dst, word_table[:].bitcast(U32).indirect(offs_sb[:, t0 // 16 : (t0 + n) // 16]))
 
@@ -101,7 +104,7 @@ def tile_picked_mixup_none_p_kernel(
             gather_words(x_code[:, t0 : t0 + n], t0, n)
         quantise_w1(1, scalar_copy)
         quantise_w1(2, scalar_copy)
-        quantise_w1(3, nc.gpsimd.tensor_copy)
+        quantise_w1(3, pool_copy)
         w2_raw = keep.tile([P, 4, N], F32, name="w2_raw", tag="raw3")
         nc.sync.dma_start(w2_raw[:], w2.rearrange("(p j) n -> p j n", j=4))
 
@@ -132,7 +135,7 @@ def tile_picked_mixup_none_p_kernel(
         w2_grouped = keep.tile([P, N * 4], BF16, name="w2_grouped", align_bytes=64)
         w2_code = keep.tile([P, N], U32, name="w2_code", align_bytes=64)
         w2_scale = keep.tile([P, N], U8, name="w2_scale", align_bytes=64)
-        nc.gpsimd.tensor_copy(w2_grouped[:].rearrange("p (n j) -> p n j", j=4), w2_raw[:].rearrange("p j n -> p n j"))
+        pool_copy(w2_grouped[:].rearrange("p (n j) -> p n j", j=4), w2_raw[:].rearrange("p j n -> p n j"))
         nc.vector.quantize_mx(w2_code[:].bitcast(FP8X4), w2_scale[:], w2_grouped[:])
 
         turns = []
@@ -200,14 +203,15 @@ def tile_picked_mixup_none_p_kernel(
 
         z = []
         for g, (b0, nb) in enumerate(GROUPS):
-            pairs = banks[g % 2][:, 0 : nb * 2 * P].rearrange("p (i u n) -> p i u n", i=nb, u=2)
+            pairs = banks[[0, 1, 0, 1, 3][g]][:, 0 : nb * 2 * P].rearrange("p (i u n) -> p i u n", i=nb, u=2)
             for i in range(nb):
                 for u in range(2):
                     nc.tensor.transpose(
                         pairs[:, i, u, :], z_t[b0 + i][:].bitcast(F32)[:, u * P : (u + 1) * P], ident[:]
                     )
             z.append(keep.tile([P, 4 * nb * P], BF16, name=f"z{g}", align_bytes=64))
-            nc.scalar.copy(
+            copy = nc.vector.tensor_copy if g == 2 else nc.scalar.copy
+            copy(
                 z[g][:].bitcast(F32).rearrange("p (i n u) -> p i n u", i=nb, u=2),
                 pairs.rearrange("p i u n -> p i n u"),
             )
@@ -217,7 +221,7 @@ def tile_picked_mixup_none_p_kernel(
             z_code = keep.tile([P, n], U32, name=f"z_code{g}", align_bytes=64)
             z_scale = keep.tile([P, n], U8, name=f"z_scale{g}", align_bytes=64)
             nc.vector.quantize_mx(z_code[:].bitcast(FP8X4), z_scale[:], z[g][:])
-            acc = banks[[4, 5, 6, 7][g]][:, 0:n]
+            acc = banks[[4, 5, 6, 7, 2][g]][:, 0:n]
             nc.tensor.matmul_mx(
                 acc,
                 lhsT=w2_code[:].bitcast(FP8X4),

@@ -24,7 +24,6 @@ TILES = H // P
 FIRST_PASSES = [(t0, 256) for t0 in range(0, S, 256)]
 DIRECT_BLOCKS = 2
 GROUPS = [(0, 2), (2, 2), (4, 2), (6, 1), (7, 1)]
-POOL_BLOCKS = 8
 
 
 def tile_picked_mixup_none_p_kernel(
@@ -39,45 +38,45 @@ def tile_picked_mixup_none_p_kernel(
 
         offs_sb = keep.tile([P, S // 16], U16, name="offs_sb")
         pos_sb = keep.tile([P, S // 16], U16, name="pos_sb")
-        scale_table = keep.tile([P, T], U8, name="scale_table", align_bytes=64)
+        scale_table = shared.tile([P, T], U8, name="scale_table", align_bytes=64, offset=4 * T)
         word_table = shared.tile([P, T], I32, name="word_table", align_bytes=64, offset=0)
         w1_raw = [keep.tile([P, 4, P], F32, name=f"w1_raw{t}", tag=f"raw{t}") for t in range(TILES)]
         share_rows = keep.tile([P, P], F32, name="share_rows")
         ident = keep.tile([P, P], F32, name="ident")
 
         nc.vector.memset(scale_table[:, 0 : T // 2].bitcast(I32), 0)
-        nc.gpsimd.memset(share_rows[:], 0.0)
         nc.gpsimd.memset(scale_table[:, T // 2 : T].bitcast(I32), 0)
         make_identity(nc, ident[:])
+        nc.scalar.activation(share_rows[:], ident[:], COPY)
 
         w1_rows = w1.rearrange("(p j) c -> p j c", j=4)
         nc.sync.dma_start(offs_sb[:], offs)
-        for r, share in enumerate((lam, mu)):
-            nc.sync.dma_start(
-                share_rows[BLOCKS * r : BLOCKS * (r + 1), :],
-                share[0:1, :].rearrange("o (b c) -> (o b) c", c=P),
-            )
+        nc.sync.dma_start(w1_raw[0][:], w1_rows[:, :, 0:P])
         for q in range(4):
             nc.sync.dma_start(
                 scale_table[32 * q : 32 * q + 4, :].bitcast(I32),
                 x_scales[0][4 * q : 4 * q + 4, :].bitcast(I32),
             )
-        nc.sync.dma_start(w1_raw[0][:], w1_rows[:, :, 0:P])
         nc.sync.dma_start(word_table[:], x_words[0].rearrange("p n t -> p (n t)").bitcast(I32))
         for t in range(1, TILES):
             nc.sync.dma_start(w1_raw[t][:], w1_rows[:, :, t * P : (t + 1) * P])
+        w2_raw = keep.tile([P, 4, N], F32, name="w2_raw")
+        nc.sync.dma_start(w2_raw[:], w2.rearrange("(p j) n -> p j n", j=4))
         nc.sync.dma_start(pos_sb[:], pos1)
+        for r, share in enumerate((lam, mu)):
+            nc.sync.dma_start(
+                share_rows[BLOCKS * r : BLOCKS * (r + 1), :],
+                share[0:1, :].rearrange("o (b c) -> (o b) c", c=P),
+            )
 
         shares = keep.tile([P, 2 * BLOCKS], F32, name="shares")
-        nc.tensor.transpose(banks[7][:, 0:P], share_rows[:], ident[:])
-        nc.scalar.activation(shares[:], banks[7][:, 0 : 2 * BLOCKS], COPY)
 
         w1_code = {}
         w1_scale = [keep.tile([P, P], U8, name=f"w1_scale{t}", align_bytes=64) for t in range(TILES)]
 
         def quantise_w1(t, copy):
             if t == 0:
-                w1_code[t] = keep.tile([P, P], U32, name=f"w1_code{t}", align_bytes=64)
+                w1_code[t] = shared.tile([P, P], U32, name=f"w1_code{t}", align_bytes=64, offset=4 * T)
             else:
                 w1_code[t] = shared.tile([P, P], U32, name=f"w1_code{t}", align_bytes=64, offset=512 * t)
             grouped = keep.tile([P, P * 4], BF16, name=f"w1_grouped{t}", align_bytes=64)
@@ -103,10 +102,8 @@ def tile_picked_mixup_none_p_kernel(
         for t0, n in FIRST_PASSES:
             gather_words(x_code[:, t0 : t0 + n], t0, n)
         quantise_w1(1, scalar_copy)
-        quantise_w1(2, scalar_copy)
+        quantise_w1(2, pool_copy)
         quantise_w1(3, pool_copy)
-        w2_raw = keep.tile([P, 4, N], F32, name="w2_raw", tag="raw3")
-        nc.sync.dma_start(w2_raw[:], w2.rearrange("(p j) n -> p j n", j=4))
 
         h = [keep.tile([P, S], F32, name=f"h{t}") for t in range(TILES)]
         passes = [(0, t0, n) for t0, n in FIRST_PASSES] + [(t, t0, BANK) for t in range(1, TILES) for t0 in (0, BANK)]
@@ -122,6 +119,9 @@ def tile_picked_mixup_none_p_kernel(
                 stop=True,
             )
             nc.scalar.copy(h[t][:, t0 : t0 + n], acc)
+            if i == 5:
+                nc.tensor.transpose(banks[2][:, 0:P], share_rows[:], ident[:])
+                nc.scalar.copy(shares[:], banks[2][:, 0 : 2 * BLOCKS])
 
         partner = {}
         for t in range(TILES):
@@ -138,12 +138,6 @@ def tile_picked_mixup_none_p_kernel(
         pool_copy(w2_grouped[:].rearrange("p (n j) -> p n j", j=4), w2_raw[:].rearrange("p j n -> p n j"))
         nc.vector.quantize_mx(w2_code[:].bitcast(FP8X4), w2_scale[:], w2_grouped[:])
 
-        turns = []
-
-        def next_bank():
-            turns.append(banks[2 + len(turns) % 6])
-            return turns[-1]
-
         def by_half(block):
             return block.rearrange("p (u half m) -> p half u m", u=2, half=2)
 
@@ -152,12 +146,11 @@ def tile_picked_mixup_none_p_kernel(
             for i, t in enumerate(tiles):
                 nc.tensor.transpose(by_tile[:, i], sources[t], ident[:])
 
-        own = []
+        own = [keep.tile([P, H], F32, name=f"own{b}") for b in range(BLOCKS)]
         z_t = [keep.tile([P, H], BF16, name=f"z_t{b}") for b in range(BLOCKS)]
         mu_of = [shares[:, BLOCKS + b : BLOCKS + b + 1] for b in range(BLOCKS)]
-        for b in range(BLOCKS):
-            h_t = next_bank()
-            own.append(keep.tile([P, H], F32, name=f"own{b}"))
+
+        def own_share(b, h_t):
             if b < DIRECT_BLOCKS:
                 for t in range(TILES):
                     nc.tensor.matmul_mx(
@@ -176,34 +169,46 @@ def tile_picked_mixup_none_p_kernel(
             nc.scalar.activation(
                 own[b][:].rearrange("p (u t m) -> p u t m", t=TILES, u=2), rows, COPY, scale=shares[:, b : b + 1]
             )
-            if b < POOL_BLOCKS:
-                low_t = next_bank()[:, 0 : H // 2]
-                turn(low_t, (0, 1), [partner[t, b] for t in range(TILES)])
-                other = keep.tile([P, 2, P], F32, name=f"other{b}")
-                nc.scalar.activation(other[:], low_t.rearrange("p (u m) -> p u m", u=2), COPY, scale=mu_of[b])
-                nc.gpsimd.tensor_tensor(by_half(z_t[b][:])[:, 0], other[:], by_half(own[b][:])[:, 0], ADD)
-        for b0 in range(0, POOL_BLOCKS, 2):
-            bank = next_bank()
+
+        def turn_partners(b, tiles, bank):
+            dst = bank[:, b % 2 * 256 : (b % 2 + 1) * 256]
+            turn(dst, tiles, [partner[t, b] for t in range(TILES)])
+            return dst.rearrange("p (u m) -> p u m", u=2)
+
+        def mix_low(b, turned):
+            other = keep.tile([P, 2, P], F32, name=f"other{b}")
+            nc.scalar.activation(other[:], turned, COPY, scale=mu_of[b])
+            nc.gpsimd.tensor_tensor(by_half(z_t[b][:])[:, 0], other[:], by_half(own[b][:])[:, 0], ADD)
+
+        def low_pair(b0, bank):
+            turned = [turn_partners(b0 + i, (0, 1), bank) for i in range(2)]
             for i in range(2):
-                turn(bank[:, i * 256 : (i + 1) * 256], (2, 3), [partner[t, b0 + i] for t in range(TILES)])
+                mix_low(b0 + i, turned[i])
+
+        own_share(0, banks[3])
+        own_share(1, banks[4])
+        own_share(2, banks[5])
+        low_pair(0, banks[0])
+        own_share(3, banks[6])
+        low_pair(2, banks[1])
+        own_share(4, banks[7])
+        own_share(5, banks[2])
+        low_pair(4, banks[3])
+        own_share(6, banks[4])
+        own_share(7, banks[5])
+        low_pair(6, banks[0])
+        for b0 in range(0, BLOCKS, 2):
+            bank = banks[[6, 1, 7, 2][b0 // 2]]
+            turned = [turn_partners(b0 + i, (2, 3), bank) for i in range(2)]
             for i in range(2):
                 b = b0 + i
                 nc.vector.scalar_tensor_tensor(
-                    by_half(z_t[b][:])[:, 1],
-                    bank[:, i * 256 : (i + 1) * 256].rearrange("p (u m) -> p u m", u=2),
-                    mu_of[b],
-                    by_half(own[b][:])[:, 1],
-                    MULT,
-                    ADD,
+                    by_half(z_t[b][:])[:, 1], turned[i], mu_of[b], by_half(own[b][:])[:, 1], MULT, ADD
                 )
-        for b in range(POOL_BLOCKS, BLOCKS):
-            partner_t = next_bank()
-            turn(partner_t[:], range(TILES), [partner[t, b] for t in range(TILES)])
-            nc.vector.scalar_tensor_tensor(z_t[b][:], partner_t[:], mu_of[b], own[b][:], MULT, ADD)
 
         z = []
         for g, (b0, nb) in enumerate(GROUPS):
-            pairs = banks[[0, 1, 0, 1, 3][g]][:, 0 : nb * 2 * P].rearrange("p (i u n) -> p i u n", i=nb, u=2)
+            pairs = banks[[3, 4, 5, 0, 6][g]][:, 0 : nb * 2 * P].rearrange("p (i u n) -> p i u n", i=nb, u=2)
             for i in range(nb):
                 for u in range(2):
                     nc.tensor.transpose(
@@ -221,7 +226,7 @@ def tile_picked_mixup_none_p_kernel(
             z_code = keep.tile([P, n], U32, name=f"z_code{g}", align_bytes=64)
             z_scale = keep.tile([P, n], U8, name=f"z_scale{g}", align_bytes=64)
             nc.vector.quantize_mx(z_code[:].bitcast(FP8X4), z_scale[:], z[g][:])
-            acc = banks[[4, 5, 6, 7, 2][g]][:, 0:n]
+            acc = banks[[1, 7, 2, 3, 4][g]][:, 0:n]
             nc.tensor.matmul_mx(
                 acc,
                 lhsT=w2_code[:].bitcast(FP8X4),

@@ -38,7 +38,7 @@ def tile_picked_mixup_none_p_kernel(
 
         offs_sb = keep.tile([P, S // 16], U16, name="offs_sb")
         pos_sb = keep.tile([P, S // 16], U16, name="pos_sb")
-        scale_table = shared.tile([P, T], U8, name="scale_table", align_bytes=64, offset=4 * T)
+        scale_table = keep.tile([P, T], U8, name="scale_table", align_bytes=64)
         word_table = shared.tile([P, T], I32, name="word_table", align_bytes=64, offset=0)
         w1_raw = [keep.tile([P, 4, P], F32, name=f"w1_raw{t}", tag=f"raw{t}") for t in range(TILES)]
         share_rows = keep.tile([P, P], F32, name="share_rows")
@@ -50,14 +50,16 @@ def tile_picked_mixup_none_p_kernel(
         nc.scalar.activation(share_rows[:], ident[:], COPY)
 
         w1_rows = w1.rearrange("(p j) c -> p j c", j=4)
-        nc.sync.dma_start(offs_sb[:], offs)
         nc.sync.dma_start(w1_raw[0][:], w1_rows[:, :, 0:P])
+        nc.sync.dma_start(offs_sb[:], offs)
+        words = x_words[0].rearrange("p n t -> p (n t)").bitcast(I32)
+        nc.sync.dma_start(word_table[:, 0 : T // 4], words[:, 0 : T // 4])
         for q in range(4):
             nc.sync.dma_start(
                 scale_table[32 * q : 32 * q + 4, :].bitcast(I32),
                 x_scales[0][4 * q : 4 * q + 4, :].bitcast(I32),
             )
-        nc.sync.dma_start(word_table[:], x_words[0].rearrange("p n t -> p (n t)").bitcast(I32))
+        nc.sync.dma_start(word_table[:, T // 4 : T], words[:, T // 4 : T])
         for t in range(1, TILES):
             nc.sync.dma_start(w1_raw[t][:], w1_rows[:, :, t * P : (t + 1) * P])
         w2_raw = keep.tile([P, 4, N], F32, name="w2_raw")
@@ -76,18 +78,21 @@ def tile_picked_mixup_none_p_kernel(
 
         def quantise_w1(t, copy):
             if t == 0:
-                w1_code[t] = shared.tile([P, P], U32, name=f"w1_code{t}", align_bytes=64, offset=4 * T)
+                w1_code[t] = keep.tile([P, P], U32, name=f"w1_code{t}", align_bytes=64)
             else:
                 w1_code[t] = shared.tile([P, P], U32, name=f"w1_code{t}", align_bytes=64, offset=512 * t)
             grouped = keep.tile([P, P * 4], BF16, name=f"w1_grouped{t}", align_bytes=64)
-            copy(
-                grouped[:].rearrange("p (u q e j) -> p q u e j", u=2, e=2, j=4),
-                w1_raw[t][:].rearrange("p j (q u e) -> p q u e j", u=2, e=2),
-            )
+            dst = grouped[:].rearrange("p (u q e j) -> p q u e j", u=2, e=2, j=4)
+            src = w1_raw[t][:].rearrange("p j (q u e) -> p q u e j", u=2, e=2)
+            copy(dst, src)
             nc.vector.quantize_mx(w1_code[t][:].bitcast(FP8X4), w1_scale[t][:], grouped[:])
 
         def scalar_copy(dst, src):
             nc.scalar.activation(dst, src, COPY)
+
+        def split_copy(dst, src):
+            nc.vector.tensor_copy(dst[:, :, 0], src[:, :, 0])
+            scalar_copy(dst[:, :, 1], src[:, :, 1])
 
         def pool_copy(dst, src):
             nc.gpsimd.tensor_scalar(dst, src, 1.0, 0.0, MULT, ADD)
@@ -96,8 +101,8 @@ def tile_picked_mixup_none_p_kernel(
             nc.vector.tensor_copy(dst, word_table[:].bitcast(U32).indirect(offs_sb[:, t0 // 16 : (t0 + n) // 16]))
 
         x_scale = keep.tile([P, S], U8, name="x_scale", align_bytes=64)
+        quantise_w1(0, split_copy)
         nc.vector.tensor_copy(x_scale[:], scale_table[:].indirect(offs_sb[:]))
-        quantise_w1(0, scalar_copy)
         x_code = keep.tile([P, S], U32, name="x_code", align_bytes=64)
         for t0, n in FIRST_PASSES:
             gather_words(x_code[:, t0 : t0 + n], t0, n)

@@ -22,7 +22,7 @@ BLOCKS = S // P
 BANK = 512
 TILES = H // P
 FIRST_PASSES = [(t0, 256) for t0 in range(0, S, 256)]
-DIRECT_BLOCKS = 2
+DIRECT_BLOCKS = (0, 1)
 GROUPS = [(0, 2), (2, 2), (4, 2), (6, 1), (7, 1)]
 
 
@@ -52,18 +52,16 @@ def tile_picked_mixup_none_p_kernel(
         w1_rows = w1.rearrange("(p j) c -> p j c", j=4)
         nc.sync.dma_start(w1_raw[0][:], w1_rows[:, :, 0:P])
         nc.sync.dma_start(offs_sb[:], offs)
-        words = x_words[0].rearrange("p n t -> p (n t)").bitcast(I32)
-        nc.sync.dma_start(word_table[:, 0 : T // 4], words[:, 0 : T // 4])
+        w2_raw = keep.tile([P, 4, N], F32, name="w2_raw")
+        nc.sync.dma_start(w2_raw[:], w2.rearrange("(p j) n -> p j n", j=4))
         for q in range(4):
             nc.sync.dma_start(
                 scale_table[32 * q : 32 * q + 4, :].bitcast(I32),
                 x_scales[0][4 * q : 4 * q + 4, :].bitcast(I32),
             )
-        nc.sync.dma_start(word_table[:, T // 4 : T], words[:, T // 4 : T])
+        nc.sync.dma_start(word_table[:], x_words[0].rearrange("p n t -> p (n t)").bitcast(I32))
         for t in range(1, TILES):
             nc.sync.dma_start(w1_raw[t][:], w1_rows[:, :, t * P : (t + 1) * P])
-        w2_raw = keep.tile([P, 4, N], F32, name="w2_raw")
-        nc.sync.dma_start(w2_raw[:], w2.rearrange("(p j) n -> p j n", j=4))
         nc.sync.dma_start(pos_sb[:], pos1)
         for r, share in enumerate((lam, mu)):
             nc.sync.dma_start(
@@ -73,19 +71,17 @@ def tile_picked_mixup_none_p_kernel(
 
         shares = keep.tile([P, 2 * BLOCKS], F32, name="shares")
 
-        w1_code = {}
-        w1_scale = [keep.tile([P, P], U8, name=f"w1_scale{t}", align_bytes=64) for t in range(TILES)]
+        w1_codes = keep.tile([P, H], U32, name="w1_codes", align_bytes=64)
+        w1_scales = keep.tile([P, H], U8, name="w1_scales", align_bytes=64)
+        w1_code = [w1_codes[:, t * P : (t + 1) * P] for t in range(TILES)]
+        w1_scale = [w1_scales[:, t * P : (t + 1) * P] for t in range(TILES)]
 
         def quantise_w1(t, copy):
-            if t == 0:
-                w1_code[t] = keep.tile([P, P], U32, name=f"w1_code{t}", align_bytes=64)
-            else:
-                w1_code[t] = shared.tile([P, P], U32, name=f"w1_code{t}", align_bytes=64, offset=512 * t)
             grouped = keep.tile([P, P * 4], BF16, name=f"w1_grouped{t}", align_bytes=64)
             dst = grouped[:].rearrange("p (u q e j) -> p q u e j", u=2, e=2, j=4)
             src = w1_raw[t][:].rearrange("p j (q u e) -> p q u e j", u=2, e=2)
             copy(dst, src)
-            nc.vector.quantize_mx(w1_code[t][:].bitcast(FP8X4), w1_scale[t][:], grouped[:])
+            nc.vector.quantize_mx(w1_code[t].bitcast(FP8X4), w1_scale[t], grouped[:])
 
         def scalar_copy(dst, src):
             nc.scalar.activation(dst, src, COPY)
@@ -103,12 +99,17 @@ def tile_picked_mixup_none_p_kernel(
         x_scale = keep.tile([P, S], U8, name="x_scale", align_bytes=64)
         quantise_w1(0, split_copy)
         nc.vector.tensor_copy(x_scale[:], scale_table[:].indirect(offs_sb[:]))
+        w2_grouped = keep.tile([P, N * 4], BF16, name="w2_grouped", align_bytes=64)
+        w2_scale = keep.tile([P, N], U8, name="w2_scale", align_bytes=64)
+        scalar_copy(w2_grouped[:].rearrange("p (n j) -> p n j", j=4), w2_raw[:].rearrange("p j n -> p n j"))
         x_code = keep.tile([P, S], U32, name="x_code", align_bytes=64)
         for t0, n in FIRST_PASSES:
             gather_words(x_code[:, t0 : t0 + n], t0, n)
         quantise_w1(1, scalar_copy)
-        quantise_w1(2, pool_copy)
+        quantise_w1(2, scalar_copy)
         quantise_w1(3, pool_copy)
+        w2_code = shared.tile([P, N], U32, name="w2_code", align_bytes=64, offset=0)
+        nc.vector.quantize_mx(w2_code[:].bitcast(FP8X4), w2_scale[:], w2_grouped[:])
 
         h = [keep.tile([P, S], F32, name=f"h{t}") for t in range(TILES)]
         passes = [(0, t0, n) for t0, n in FIRST_PASSES] + [(t, t0, BANK) for t in range(1, TILES) for t0 in (0, BANK)]
@@ -116,8 +117,8 @@ def tile_picked_mixup_none_p_kernel(
             acc = banks[i % 8][:, 0:n]
             nc.tensor.matmul_mx(
                 acc,
-                lhsT=w1_code[t][:].bitcast(FP8X4),
-                lhsT_scale=w1_scale[t][:],
+                lhsT=w1_code[t].bitcast(FP8X4),
+                lhsT_scale=w1_scale[t],
                 rhs=x_code[:, t0 : t0 + n].bitcast(FP8X4),
                 rhs_scale=x_scale[:, t0 : t0 + n],
                 start=True,
@@ -137,12 +138,6 @@ def tile_picked_mixup_none_p_kernel(
                 for i in range(n // P):
                     partner[t, t0 // P + i] = piece[:, i * P : (i + 1) * P]
 
-        w2_grouped = keep.tile([P, N * 4], BF16, name="w2_grouped", align_bytes=64)
-        w2_code = keep.tile([P, N], U32, name="w2_code", align_bytes=64)
-        w2_scale = keep.tile([P, N], U8, name="w2_scale", align_bytes=64)
-        pool_copy(w2_grouped[:].rearrange("p (n j) -> p n j", j=4), w2_raw[:].rearrange("p j n -> p n j"))
-        nc.vector.quantize_mx(w2_code[:].bitcast(FP8X4), w2_scale[:], w2_grouped[:])
-
         def by_half(block):
             return block.rearrange("p (u half m) -> p half u m", u=2, half=2)
 
@@ -156,17 +151,16 @@ def tile_picked_mixup_none_p_kernel(
         mu_of = [shares[:, BLOCKS + b : BLOCKS + b + 1] for b in range(BLOCKS)]
 
         def own_share(b, h_t):
-            if b < DIRECT_BLOCKS:
-                for t in range(TILES):
-                    nc.tensor.matmul_mx(
-                        h_t[:, t * P : (t + 1) * P],
-                        lhsT=x_code[:, b * P : (b + 1) * P].bitcast(FP8X4),
-                        lhsT_scale=x_scale[:, b * P : (b + 1) * P],
-                        rhs=w1_code[t][:].bitcast(FP8X4),
-                        rhs_scale=w1_scale[t][:],
-                        start=True,
-                        stop=True,
-                    )
+            if b in DIRECT_BLOCKS:
+                nc.tensor.matmul_mx(
+                    h_t[:],
+                    lhsT=x_code[:, b * P : (b + 1) * P].bitcast(FP8X4),
+                    lhsT_scale=x_scale[:, b * P : (b + 1) * P],
+                    rhs=w1_codes[:].bitcast(FP8X4),
+                    rhs_scale=w1_scales[:],
+                    start=True,
+                    stop=True,
+                )
                 rows = h_t[:].rearrange("p (t u m) -> p u t m", t=TILES, u=2)
             else:
                 turn(h_t[:], range(TILES), [h[t][:, b * P : (b + 1) * P] for t in range(TILES)])
@@ -185,23 +179,14 @@ def tile_picked_mixup_none_p_kernel(
             nc.scalar.activation(other[:], turned, COPY, scale=mu_of[b])
             nc.gpsimd.tensor_tensor(by_half(z_t[b][:])[:, 0], other[:], by_half(own[b][:])[:, 0], ADD)
 
-        def low_pair(b0, bank):
-            turned = [turn_partners(b0 + i, (0, 1), bank) for i in range(2)]
-            for i in range(2):
-                mix_low(b0 + i, turned[i])
-
-        own_share(0, banks[3])
-        own_share(1, banks[4])
-        own_share(2, banks[5])
-        low_pair(0, banks[0])
-        own_share(3, banks[6])
-        low_pair(2, banks[1])
-        own_share(4, banks[7])
-        own_share(5, banks[2])
-        low_pair(4, banks[3])
-        own_share(6, banks[4])
-        own_share(7, banks[5])
-        low_pair(6, banks[0])
+        own_banks = [3, 4, 5, 6, 7, 2, 4, 5]
+        low_banks = [0, 1, 3, 0]
+        for b0 in range(0, BLOCKS, 2):
+            own_share(b0, banks[own_banks[b0]])
+            turned = [turn_partners(b0 + i, (0, 1), banks[low_banks[b0 // 2]]) for i in range(2)]
+            mix_low(b0, turned[0])
+            own_share(b0 + 1, banks[own_banks[b0 + 1]])
+            mix_low(b0 + 1, turned[1])
         for b0 in range(0, BLOCKS, 2):
             bank = banks[[6, 1, 7, 2][b0 // 2]]
             turned = [turn_partners(b0 + i, (2, 3), bank) for i in range(2)]

@@ -22,7 +22,7 @@ BLOCKS = S // P
 BANK = 512
 TILES = H // P
 FIRST_PASSES = [(t0, 256) for t0 in range(0, S, 256)]
-DIRECT_BLOCKS = (0, 1)
+DIRECT_BLOCKS = (6, 7)
 GROUPS = [(0, 2), (2, 2), (4, 2), (6, 1), (7, 1)]
 
 

@@ -1,7 +1,6 @@
 from contextlib import ExitStack
 
 import concourse.mybir as mybir
-from concourse.masks import make_identity
 
 K, T, S, H, N = 512, 2048, 1024, 512, 128
 FLOPS = 2 * K * H * S + 2 * H * N * S
@@ -18,12 +17,11 @@ MULT = mybir.AluOpType.mult
 ADD = mybir.AluOpType.add
 
 P = 128
-BLOCKS = S // P
 BANK = 512
 TILES = H // P
-FIRST_PASSES = [(t0, 256) for t0 in range(0, S, 256)]
-DIRECT_BLOCKS = (6, 7)
-GROUPS = [(0, 2), (2, 2), (4, 2), (6, 1), (7, 1)]
+PIECE = 256
+HALF = H // 2
+ROUNDS = [(0, 128, True), (128, 256, False), (384, 256, False), (640, 256, False), (896, 128, False)]
 
 
 def tile_picked_mixup_none_p_kernel(
@@ -32,191 +30,119 @@ def tile_picked_mixup_none_p_kernel(
     nc = tc.nc
     with ExitStack() as ctx:
         keep = ctx.enter_context(tc.tile_pool(name="keep", bufs=1))
-        shared = ctx.enter_context(tc.tile_pool(name="shared", bufs=1))
         psum = ctx.enter_context(tc.psum_pool(name="psum", bufs=1))
         banks = [psum.tile([P, BANK], F32, name=f"bank{i}") for i in range(8)]
 
         offs_sb = keep.tile([P, S // 16], U16, name="offs_sb")
         pos_sb = keep.tile([P, S // 16], U16, name="pos_sb")
         scale_table = keep.tile([P, T], U8, name="scale_table", align_bytes=64)
-        word_table = shared.tile([P, T], I32, name="word_table", align_bytes=64, offset=0)
-        w1_raw = [keep.tile([P, 4, P], F32, name=f"w1_raw{t}", tag=f"raw{t}") for t in range(TILES)]
-        share_rows = keep.tile([P, P], F32, name="share_rows")
-        ident = keep.tile([P, P], F32, name="ident")
+        word_table = keep.tile([P, T], I32, name="word_table", align_bytes=64)
+        w1_raw = [keep.tile([P, 4, HALF], F32, name=f"w1_raw{i}") for i in range(2)]
+        w2_raw = keep.tile([P, 4, N], F32, name="w2_raw")
+        lam_sb = keep.tile([P, S], F32, name="lam_sb")
+        mu_sb = keep.tile([P, S], F32, name="mu_sb")
 
         nc.vector.memset(scale_table[:, 0 : T // 2].bitcast(I32), 0)
         nc.gpsimd.memset(scale_table[:, T // 2 : T].bitcast(I32), 0)
-        make_identity(nc, ident[:])
-        nc.scalar.activation(share_rows[:], ident[:], COPY)
 
         w1_rows = w1.rearrange("(p j) c -> p j c", j=4)
-        nc.sync.dma_start(w1_raw[0][:], w1_rows[:, :, 0:P])
+        nc.sync.dma_start(w1_raw[0][:], w1_rows[:, :, 0:HALF])
         nc.sync.dma_start(offs_sb[:], offs)
-        w2_raw = keep.tile([P, 4, N], F32, name="w2_raw")
-        nc.sync.dma_start(w2_raw[:], w2.rearrange("(p j) n -> p j n", j=4))
         for q in range(4):
             nc.sync.dma_start(
                 scale_table[32 * q : 32 * q + 4, :].bitcast(I32),
                 x_scales[0][4 * q : 4 * q + 4, :].bitcast(I32),
             )
         nc.sync.dma_start(word_table[:], x_words[0].rearrange("p n t -> p (n t)").bitcast(I32))
-        for t in range(1, TILES):
-            nc.sync.dma_start(w1_raw[t][:], w1_rows[:, :, t * P : (t + 1) * P])
+        nc.sync.dma_start(w1_raw[1][:], w1_rows[:, :, HALF:H])
         nc.sync.dma_start(pos_sb[:], pos1)
-        for r, share in enumerate((lam, mu)):
-            nc.sync.dma_start(
-                share_rows[BLOCKS * r : BLOCKS * (r + 1), :],
-                share[0:1, :].rearrange("o (b c) -> (o b) c", c=P),
+        nc.sync.dma_start(w2_raw[:], w2.rearrange("(p j) n -> p j n", j=4))
+        nc.sync.dma_start(lam_sb[:], lam)
+        nc.sync.dma_start(mu_sb[:], mu)
+
+        w1_grouped = keep.tile([P, TILES, P, 4], BF16, name="w1_grouped", align_bytes=64)
+        for i in range(2):
+            nc.scalar.activation(
+                w1_grouped[:, :, i * P // 2 : (i + 1) * P // 2, :].rearrange("p t m j -> p m j t"),
+                w1_raw[i][:].rearrange("p j (m t) -> p m j t", t=TILES),
+                COPY,
             )
-
-        shares = keep.tile([P, 2 * BLOCKS], F32, name="shares")
-
-        w1_codes = keep.tile([P, H], U32, name="w1_codes", align_bytes=64)
-        w1_scales = keep.tile([P, H], U8, name="w1_scales", align_bytes=64)
-        w1_code = [w1_codes[:, t * P : (t + 1) * P] for t in range(TILES)]
-        w1_scale = [w1_scales[:, t * P : (t + 1) * P] for t in range(TILES)]
-
-        def quantise_w1(t, copy):
-            grouped = keep.tile([P, P * 4], BF16, name=f"w1_grouped{t}", align_bytes=64)
-            dst = grouped[:].rearrange("p (u q e j) -> p q u e j", u=2, e=2, j=4)
-            src = w1_raw[t][:].rearrange("p j (q u e) -> p q u e j", u=2, e=2)
-            copy(dst, src)
-            nc.vector.quantize_mx(w1_code[t].bitcast(FP8X4), w1_scale[t], grouped[:])
-
-        def scalar_copy(dst, src):
-            nc.scalar.activation(dst, src, COPY)
-
-        def split_copy(dst, src):
-            nc.vector.tensor_copy(dst[:, :, 0], src[:, :, 0])
-            scalar_copy(dst[:, :, 1], src[:, :, 1])
-
-        def pool_copy(dst, src):
-            nc.gpsimd.tensor_scalar(dst, src, 1.0, 0.0, MULT, ADD)
-
-        def gather_words(dst, t0, n):
-            nc.vector.tensor_copy(dst, word_table[:].bitcast(U32).indirect(offs_sb[:, t0 // 16 : (t0 + n) // 16]))
+        w2_grouped = keep.tile([P, N * 4], BF16, name="w2_grouped", align_bytes=64)
+        nc.scalar.activation(
+            w2_grouped[:].rearrange("p (c i j) -> p c j i", i=4, j=4),
+            w2_raw[:].rearrange("p j (c i) -> p c j i", i=4),
+            COPY,
+        )
 
         x_scale = keep.tile([P, S], U8, name="x_scale", align_bytes=64)
-        quantise_w1(0, split_copy)
         nc.vector.tensor_copy(x_scale[:], scale_table[:].indirect(offs_sb[:]))
-        w2_grouped = keep.tile([P, N * 4], BF16, name="w2_grouped", align_bytes=64)
-        w2_scale = keep.tile([P, N], U8, name="w2_scale", align_bytes=64)
-        scalar_copy(w2_grouped[:].rearrange("p (n j) -> p n j", j=4), w2_raw[:].rearrange("p j n -> p n j"))
         x_code = keep.tile([P, S], U32, name="x_code", align_bytes=64)
-        for t0, n in FIRST_PASSES:
-            gather_words(x_code[:, t0 : t0 + n], t0, n)
-        quantise_w1(1, scalar_copy)
-        quantise_w1(2, scalar_copy)
-        quantise_w1(3, pool_copy)
-        w2_code = shared.tile([P, N], U32, name="w2_code", align_bytes=64, offset=0)
+        for t0 in range(0, S, BANK):
+            nc.vector.tensor_copy(
+                x_code[:, t0 : t0 + BANK],
+                word_table[:].bitcast(U32).indirect(offs_sb[:, t0 // 16 : (t0 + BANK) // 16]),
+            )
+        w1_codes = keep.tile([P, H], U32, name="w1_codes", align_bytes=64)
+        w1_scales = keep.tile([P, H], U8, name="w1_scales", align_bytes=64)
+        w1_flat = w1_grouped[:].rearrange("p t m j -> p (t m j)")
+        for c0, c1 in ((0, P), (P, 2 * P), (2 * P, H)):
+            nc.vector.quantize_mx(w1_codes[:, c0:c1].bitcast(FP8X4), w1_scales[:, c0:c1], w1_flat[:, 4 * c0 : 4 * c1])
+        w2_code = keep.tile([P, N], U32, name="w2_code", align_bytes=64)
+        w2_scale = keep.tile([P, N], U8, name="w2_scale", align_bytes=64)
         nc.vector.quantize_mx(w2_code[:].bitcast(FP8X4), w2_scale[:], w2_grouped[:])
 
         h = [keep.tile([P, S], F32, name=f"h{t}") for t in range(TILES)]
-        passes = [(0, t0, n) for t0, n in FIRST_PASSES] + [(t, t0, BANK) for t in range(1, TILES) for t0 in (0, BANK)]
-        for i, (t, t0, n) in enumerate(passes):
-            acc = banks[i % 8][:, 0:n]
-            nc.tensor.matmul_mx(
-                acc,
-                lhsT=w1_code[t].bitcast(FP8X4),
-                lhsT_scale=w1_scale[t],
-                rhs=x_code[:, t0 : t0 + n].bitcast(FP8X4),
-                rhs_scale=x_scale[:, t0 : t0 + n],
-                start=True,
-                stop=True,
-            )
-            nc.scalar.copy(h[t][:, t0 : t0 + n], acc)
-            if i == 5:
-                nc.tensor.transpose(banks[2][:, 0:P], share_rows[:], ident[:])
-                nc.scalar.copy(shares[:], banks[2][:, 0 : 2 * BLOCKS])
-
-        partner = {}
+        own = keep.tile([P, TILES, S], F32, name="own")
         for t in range(TILES):
-            n = 256 if t == TILES - 1 else 512
-            for t0 in range(0, S, n):
-                piece = keep.tile([P, n], F32, name=f"partner{t}_{t0}")
-                nc.vector.tensor_copy(piece[:], h[t][:].indirect(pos_sb[:, t0 // 16 : (t0 + n) // 16]))
-                for i in range(n // P):
-                    partner[t, t0 // P + i] = piece[:, i * P : (i + 1) * P]
-
-        def by_half(block):
-            return block.rearrange("p (u half m) -> p half u m", u=2, half=2)
-
-        def turn(dst, tiles, sources):
-            by_tile = dst.rearrange("p (u t m) -> p t u m", u=2, t=len(tiles))
-            for i, t in enumerate(tiles):
-                nc.tensor.transpose(by_tile[:, i], sources[t], ident[:])
-
-        own = [keep.tile([P, H], F32, name=f"own{b}") for b in range(BLOCKS)]
-        z_t = [keep.tile([P, H], BF16, name=f"z_t{b}") for b in range(BLOCKS)]
-        mu_of = [shares[:, BLOCKS + b : BLOCKS + b + 1] for b in range(BLOCKS)]
-
-        def own_share(b, h_t):
-            if b in DIRECT_BLOCKS:
+            for i, t0 in enumerate((0, BANK)):
+                acc = banks[2 * t + i][:]
+                cols = slice(t0, t0 + BANK)
                 nc.tensor.matmul_mx(
-                    h_t[:],
-                    lhsT=x_code[:, b * P : (b + 1) * P].bitcast(FP8X4),
-                    lhsT_scale=x_scale[:, b * P : (b + 1) * P],
-                    rhs=w1_codes[:].bitcast(FP8X4),
-                    rhs_scale=w1_scales[:],
+                    acc,
+                    lhsT=w1_codes[:, t * P : (t + 1) * P].bitcast(FP8X4),
+                    lhsT_scale=w1_scales[:, t * P : (t + 1) * P],
+                    rhs=x_code[:, cols].bitcast(FP8X4),
+                    rhs_scale=x_scale[:, cols],
                     start=True,
                     stop=True,
                 )
-                rows = h_t[:].rearrange("p (t u m) -> p u t m", t=TILES, u=2)
+                nc.scalar.copy(h[t][:, cols], acc)
+                nc.vector.tensor_tensor(own[:, t, cols], acc, lam_sb[:, cols], MULT)
+
+        other = {}
+        z = {}
+
+        def gather(r):
+            s0, n, fused = ROUNDS[r]
+            cols = pos_sb[:, s0 // 16 : (s0 + n) // 16]
+            other[r] = keep.tile([P, TILES, n], F32, name=f"other{r}")
+            if fused:
+                for t in range(TILES):
+                    nc.vector.tensor_tensor(other[r][:, t, :], h[t][:].indirect(cols), mu_sb[:, s0 : s0 + n], MULT)
             else:
-                turn(h_t[:], range(TILES), [h[t][:, b * P : (b + 1) * P] for t in range(TILES)])
-                rows = h_t[:].rearrange("p (u t m) -> p u t m", t=TILES, u=2)
-            nc.scalar.activation(
-                own[b][:].rearrange("p (u t m) -> p u t m", t=TILES, u=2), rows, COPY, scale=shares[:, b : b + 1]
-            )
-
-        def turn_partners(b, tiles, bank):
-            dst = bank[:, b % 2 * 256 : (b % 2 + 1) * 256]
-            turn(dst, tiles, [partner[t, b] for t in range(TILES)])
-            return dst.rearrange("p (u m) -> p u m", u=2)
-
-        def mix_low(b, turned):
-            other = keep.tile([P, 2, P], F32, name=f"other{b}")
-            nc.scalar.activation(other[:], turned, COPY, scale=mu_of[b])
-            nc.gpsimd.tensor_tensor(by_half(z_t[b][:])[:, 0], other[:], by_half(own[b][:])[:, 0], ADD)
-
-        own_banks = [3, 4, 5, 6, 7, 2, 4, 5]
-        low_banks = [0, 1, 3, 0]
-        for b0 in range(0, BLOCKS, 2):
-            own_share(b0, banks[own_banks[b0]])
-            turned = [turn_partners(b0 + i, (0, 1), banks[low_banks[b0 // 2]]) for i in range(2)]
-            mix_low(b0, turned[0])
-            own_share(b0 + 1, banks[own_banks[b0 + 1]])
-            mix_low(b0 + 1, turned[1])
-        for b0 in range(0, BLOCKS, 2):
-            bank = banks[[6, 1, 7, 2][b0 // 2]]
-            turned = [turn_partners(b0 + i, (2, 3), bank) for i in range(2)]
-            for i in range(2):
-                b = b0 + i
-                nc.vector.scalar_tensor_tensor(
-                    by_half(z_t[b][:])[:, 1], turned[i], mu_of[b], by_half(own[b][:])[:, 1], MULT, ADD
+                partner = keep.tile([P, TILES, n], F32, name=f"partner{r}")
+                for t in range(TILES):
+                    nc.scalar.activation(partner[:, t, :], h[t][:].indirect(cols), COPY)
+                nc.vector.tensor_tensor(
+                    other[r][:], partner[:], mu_sb[:, s0 : s0 + n].unsqueeze(1).broadcast_to([P, TILES, n]), MULT
                 )
 
-        z = []
-        for g, (b0, nb) in enumerate(GROUPS):
-            pairs = banks[[3, 4, 5, 0, 6][g]][:, 0 : nb * 2 * P].rearrange("p (i u n) -> p i u n", i=nb, u=2)
-            for i in range(nb):
-                for u in range(2):
-                    nc.tensor.transpose(
-                        pairs[:, i, u, :], z_t[b0 + i][:].bitcast(F32)[:, u * P : (u + 1) * P], ident[:]
-                    )
-            z.append(keep.tile([P, 4 * nb * P], BF16, name=f"z{g}", align_bytes=64))
-            copy = nc.vector.tensor_copy if g == 2 else nc.scalar.copy
-            copy(
-                z[g][:].bitcast(F32).rearrange("p (i n u) -> p i n u", i=nb, u=2),
-                pairs.rearrange("p i u n -> p i n u"),
+        def mix(r):
+            s0, n, fused = ROUNDS[r]
+            z[r] = keep.tile([P, 4 * n], BF16, name=f"z{r}", align_bytes=64)
+            nc.vector.tensor_tensor(
+                z[r][:].rearrange("p (c i t) -> p c t i", i=4, t=TILES),
+                other[r][:].rearrange("p t (c i) -> p c t i", i=4),
+                own[:, :, s0 : s0 + n].rearrange("p t (c i) -> p c t i", i=4),
+                ADD,
             )
 
-        for g, (b0, nb) in enumerate(GROUPS):
-            n = nb * P
-            z_code = keep.tile([P, n], U32, name=f"z_code{g}", align_bytes=64)
-            z_scale = keep.tile([P, n], U8, name=f"z_scale{g}", align_bytes=64)
-            nc.vector.quantize_mx(z_code[:].bitcast(FP8X4), z_scale[:], z[g][:])
-            acc = banks[[1, 7, 2, 3, 4][g]][:, 0:n]
+        def second_layer(r):
+            s0, n, fused = ROUNDS[r]
+            z_code = keep.tile([P, n], U32, name=f"z_code{r}", align_bytes=64)
+            z_scale = keep.tile([P, n], U8, name=f"z_scale{r}", align_bytes=64)
+            nc.vector.quantize_mx(z_code[:].bitcast(FP8X4), z_scale[:], z[r][:])
+            acc = banks[r][:, 0:n]
             nc.tensor.matmul_mx(
                 acc,
                 lhsT=w2_code[:].bitcast(FP8X4),
@@ -226,9 +152,14 @@ def tile_picked_mixup_none_p_kernel(
                 start=True,
                 stop=True,
             )
-            res = keep.tile([P, n], F32, name=f"res{g}")
-            if g < 3:
-                nc.scalar.copy(res[:], acc)
-            else:
-                nc.vector.tensor_copy(res[:], acc)
-            nc.sync.dma_start(out[:, b0 * P : b0 * P + n], res[:])
+            res = keep.tile([P, n], F32, name=f"res{r}")
+            nc.scalar.copy(res[:], acc)
+            nc.sync.dma_start(out[:, s0 : s0 + n], res[:])
+
+        for r in range(len(ROUNDS) + 1):
+            if r < len(ROUNDS):
+                gather(r)
+            if r >= 1:
+                second_layer(r - 1)
+            if r < len(ROUNDS):
+                mix(r)

@@ -1,6 +1,7 @@
 from contextlib import ExitStack
 
 import concourse.mybir as mybir
+from concourse.masks import make_identity
 
 K, T, S, H, N = 512, 2048, 1024, 512, 128
 FLOPS = 2 * K * H * S + 2 * H * N * S
@@ -20,8 +21,9 @@ P = 128
 BANK = 512
 TILES = H // P
 PIECE = 256
-HALF = H // 2
-ROUNDS = [(0, 128, True), (128, 256, False), (384, 256, False), (640, 256, False), (896, 128, False)]
+LOW = 512
+TURNED = (S - LOW) // P
+ROUNDS = [(0, 256), (256, 128), (384, 128)]
 
 
 def tile_picked_mixup_none_p_kernel(
@@ -30,43 +32,75 @@ def tile_picked_mixup_none_p_kernel(
     nc = tc.nc
     with ExitStack() as ctx:
         keep = ctx.enter_context(tc.tile_pool(name="keep", bufs=1))
+        shared = ctx.enter_context(tc.tile_pool(name="shared", bufs=1))
         psum = ctx.enter_context(tc.psum_pool(name="psum", bufs=1))
         banks = [psum.tile([P, BANK], F32, name=f"bank{i}") for i in range(8)]
 
         offs_sb = keep.tile([P, S // 16], U16, name="offs_sb")
         pos_sb = keep.tile([P, S // 16], U16, name="pos_sb")
         scale_table = keep.tile([P, T], U8, name="scale_table", align_bytes=64)
-        word_table = keep.tile([P, T], I32, name="word_table", align_bytes=64)
-        w1_raw = [keep.tile([P, 4, HALF], F32, name=f"w1_raw{i}") for i in range(2)]
+        word_table = shared.tile([P, T], I32, name="word_table", align_bytes=64, offset=10240)
+        w1_raw = keep.tile([P, 4, H], F32, name="w1_raw")
         w2_raw = keep.tile([P, 4, N], F32, name="w2_raw")
-        lam_sb = keep.tile([P, S], F32, name="lam_sb")
-        mu_sb = keep.tile([P, S], F32, name="mu_sb")
+        lam_sb = keep.tile([P, LOW], F32, name="lam_sb")
+        mu_sb = keep.tile([P, LOW], F32, name="mu_sb")
+        share_rows = keep.tile([P, P], F32, name="share_rows")
+        ident = keep.tile([P, P], F32, name="ident")
 
         nc.vector.memset(scale_table[:, 0 : T // 2].bitcast(I32), 0)
         nc.gpsimd.memset(scale_table[:, T // 2 : T].bitcast(I32), 0)
+        make_identity(nc, ident[:])
 
+        for r, share in enumerate((lam, mu)):
+            nc.sync.dma_start(
+                share_rows[P // 2 * r : P // 2 * (r + 1), :],
+                share[0 : P // 2 // TURNED, LOW:S].rearrange("o (b c) -> o b c", c=P),
+            )
         w1_rows = w1.rearrange("(p j) c -> p j c", j=4)
-        nc.sync.dma_start(w1_raw[0][:], w1_rows[:, :, 0:HALF])
+        nc.sync.dma_start(w1_raw[:, 0:3, :], w1_rows[:, 0:3, :])
         nc.sync.dma_start(offs_sb[:], offs)
         for q in range(4):
             nc.sync.dma_start(
                 scale_table[32 * q : 32 * q + 4, :].bitcast(I32),
                 x_scales[0][4 * q : 4 * q + 4, :].bitcast(I32),
             )
+        nc.sync.dma_start(w1_raw[:, 3:4, :], w1_rows[:, 3:4, :])
         nc.sync.dma_start(word_table[:], x_words[0].rearrange("p n t -> p (n t)").bitcast(I32))
-        nc.sync.dma_start(w1_raw[1][:], w1_rows[:, :, HALF:H])
-        nc.sync.dma_start(pos_sb[:], pos1)
         nc.sync.dma_start(w2_raw[:], w2.rearrange("(p j) n -> p j n", j=4))
-        nc.sync.dma_start(lam_sb[:], lam)
-        nc.sync.dma_start(mu_sb[:], mu)
+        nc.sync.dma_start(lam_sb[:], lam[:, 0:LOW])
+        nc.sync.dma_start(pos_sb[:], pos1)
+        nc.sync.dma_start(mu_sb[:], mu[:, 0:LOW])
 
-        w1_grouped = keep.tile([P, TILES, P, 4], BF16, name="w1_grouped", align_bytes=64)
+        nc.tensor.transpose(banks[6][:, 0:P], share_rows[:], ident[:])
+        lam_col = banks[6][:, 0:TURNED]
+        mu_col = banks[6][:, P // 2 : P // 2 + TURNED]
+        nudge_tile = shared.tile([P, 32], F32, name="nudge_tile", align_bytes=64, offset=4096 - 64)
+        nudge = nudge_tile[:, 0:TURNED]
+        pivot = keep.tile([P, TURNED], F32, name="pivot")
+        inverse_tile = shared.tile([P, 32], F32, name="inverse_tile", align_bytes=64, offset=7168 - 64)
+        inverse = inverse_tile[:, 0:TURNED]
+        ratio_col = keep.tile([P, TURNED], F32, name="ratio_col")
+        nc.scalar.activation(nudge, mu_col, COPY, bias=2.0**-100, scale=2.0**-40)
+        nc.vector.tensor_tensor(pivot[:], lam_col, nudge, ADD)
+        nc.vector.reciprocal(inverse, pivot[:])
+        nc.vector.tensor_tensor(ratio_col[:], mu_col, inverse, MULT)
+        for b in range(TURNED):
+            nc.tensor.transpose(
+                banks[7][:, b * P : (b + 1) * P], ratio_col[:, b : b + 1].to_broadcast([P, P]), ident[:]
+            )
+
+        w1_grouped = [
+            shared.tile([P, 2, P, 4], BF16, name=f"w1_grouped{i}", align_bytes=64, offset=2048 * (i + 1))
+            for i in range(2)
+        ]
         for i in range(2):
             nc.scalar.activation(
-                w1_grouped[:, :, i * P // 2 : (i + 1) * P // 2, :].rearrange("p t m j -> p m j t"),
-                w1_raw[i][:].rearrange("p j (m t) -> p m j t", t=TILES),
+                w1_grouped[i][:].rearrange("p t m j -> p m j t"),
+                w1_raw[:].rearrange("p j (m t) -> p m j t", t=TILES)[:, :, :, 2 * i : 2 * i + 2],
                 COPY,
             )
+        ratio = keep.tile([P, S - LOW], F32, name="ratio")
+        nc.scalar.copy(ratio[:], banks[7][:])
         w2_grouped = keep.tile([P, N * 4], BF16, name="w2_grouped", align_bytes=64)
         nc.scalar.activation(
             w2_grouped[:].rearrange("p (c i j) -> p c j i", i=4, j=4),
@@ -74,75 +108,148 @@ def tile_picked_mixup_none_p_kernel(
             COPY,
         )
 
-        x_scale = keep.tile([P, S], U8, name="x_scale", align_bytes=64)
-        nc.vector.tensor_copy(x_scale[:], scale_table[:].indirect(offs_sb[:]))
-        x_code = keep.tile([P, S], U32, name="x_code", align_bytes=64)
-        for t0 in range(0, S, BANK):
-            nc.vector.tensor_copy(
-                x_code[:, t0 : t0 + BANK],
-                word_table[:].bitcast(U32).indirect(offs_sb[:, t0 // 16 : (t0 + BANK) // 16]),
-            )
-        w1_codes = keep.tile([P, H], U32, name="w1_codes", align_bytes=64)
+        x_code = shared.tile([P, S], U32, name="x_code", align_bytes=64, offset=0)
+        w1_codes = [
+            shared.tile([P, 2 * P], U32, name=f"w1_codes{i}", align_bytes=64, offset=(6144, 10240)[i]) for i in range(2)
+        ]
+        x_scale = shared.tile([P, S], U8, name="x_scale", align_bytes=64, offset=7168)
         w1_scales = keep.tile([P, H], U8, name="w1_scales", align_bytes=64)
-        w1_flat = w1_grouped[:].rearrange("p t m j -> p (t m j)")
-        for c0, c1 in ((0, P), (P, 2 * P), (2 * P, H)):
-            nc.vector.quantize_mx(w1_codes[:, c0:c1].bitcast(FP8X4), w1_scales[:, c0:c1], w1_flat[:, 4 * c0 : 4 * c1])
+
+        def quantise_w1(i):
+            cols = slice(2 * P * i, 2 * P * (i + 1))
+            nc.vector.quantize_mx(
+                w1_codes[i][:].bitcast(FP8X4), w1_scales[:, cols], w1_grouped[i][:].rearrange("p t m j -> p (t m j)")
+            )
+
+        nc.vector.tensor_copy(x_scale[:], scale_table[:].indirect(offs_sb[:]))
+        quantise_w1(0)
+        for t0 in range(0, S, PIECE):
+            nc.vector.tensor_copy(
+                x_code[:, t0 : t0 + PIECE],
+                word_table[:].bitcast(U32).indirect(offs_sb[:, t0 // 16 : (t0 + PIECE) // 16]),
+            )
+        quantise_w1(1)
+
+        h = [keep.tile([P, S], F32, name=f"h{t}") for t in range(TILES)]
+        own = keep.tile([P, TILES, LOW], F32, name="own")
+        fills = [((0, 1), t0, PIECE) for t0 in range(0, S, PIECE)]
+        fills = fills + [((t,), t0, BANK) for t in (2, 3) for t0 in (0, BANK)]
+
+        def own_share(i):
+            tiles, t0, n = fills[i]
+            nc.vector.tensor_tensor(
+                own[:, tiles[0] : tiles[-1] + 1, t0 : t0 + n],
+                banks[i][:].rearrange("p (i n) -> p i n", n=n),
+                lam_sb[:, t0 : t0 + n].unsqueeze(1).broadcast_to([P, len(tiles), n]),
+                MULT,
+            )
+
+        for i, (tiles, t0, n) in enumerate(fills):
+            for j, t in enumerate(tiles):
+                nc.tensor.matmul_mx(
+                    banks[i][:, j * n : (j + 1) * n],
+                    lhsT=w1_codes[t // 2][:, t % 2 * P : (t % 2 + 1) * P].bitcast(FP8X4),
+                    lhsT_scale=w1_scales[:, t * P : (t + 1) * P],
+                    rhs=x_code[:, t0 : t0 + n].bitcast(FP8X4),
+                    rhs_scale=x_scale[:, t0 : t0 + n],
+                    start=True,
+                    stop=True,
+                )
+            for j, t in enumerate(tiles):
+                nc.scalar.copy(h[t][:, t0 : t0 + n], banks[i][:, j * n : (j + 1) * n])
+        own_share(0)
+        own_share(1)
+
+        scaled = [keep.tile([P, S - LOW], F32, name=f"scaled{t}") for t in range(TILES)]
+
+        def gather_scaled(t, c0, n):
+            nc.vector.tensor_tensor(
+                scaled[t][:, c0 : c0 + n],
+                h[t][:].indirect(pos_sb[:, (LOW + c0) // 16 : (LOW + c0 + n) // 16]),
+                ratio[:, c0 : c0 + n],
+                MULT,
+            )
+
+        gather_scaled(0, 0, 512)
+        gather_scaled(1, 0, 512)
+        own_share(4)
+        gather_scaled(2, 0, 512)
+        gather_scaled(3, 0, 256)
+        gather_scaled(3, 256, 256)
+        own_share(6)
         w2_code = keep.tile([P, N], U32, name="w2_code", align_bytes=64)
         w2_scale = keep.tile([P, N], U8, name="w2_scale", align_bytes=64)
         nc.vector.quantize_mx(w2_code[:].bitcast(FP8X4), w2_scale[:], w2_grouped[:])
 
-        h = [keep.tile([P, S], F32, name=f"h{t}") for t in range(TILES)]
-        own = keep.tile([P, TILES, S], F32, name="own")
-        for t in range(TILES):
-            for i, t0 in enumerate((0, BANK)):
-                acc = banks[2 * t + i][:]
-                cols = slice(t0, t0 + BANK)
-                nc.tensor.matmul_mx(
-                    acc,
-                    lhsT=w1_codes[:, t * P : (t + 1) * P].bitcast(FP8X4),
-                    lhsT_scale=w1_scales[:, t * P : (t + 1) * P],
-                    rhs=x_code[:, cols].bitcast(FP8X4),
-                    rhs_scale=x_scale[:, cols],
-                    start=True,
-                    stop=True,
-                )
-                nc.scalar.copy(h[t][:, cols], acc)
-                nc.vector.tensor_tensor(own[:, t, cols], acc, lam_sb[:, cols], MULT)
+        partner = []
+        for r, (s0, n) in enumerate(ROUNDS):
+            partner.append(
+                shared.tile([P, TILES, n], F32, name=f"partner{r}", align_bytes=64, offset=(0, 10240, 7168)[r])
+            )
+            for t in range(TILES):
+                nc.scalar.activation(partner[r][:, t, :], h[t][:].indirect(pos_sb[:, s0 // 16 : (s0 + n) // 16]), COPY)
 
-        other = {}
+        sums = [banks[i] for i in (2, 3, 5, 7)]
+        for half, source in enumerate(([h[t][:, LOW:S] for t in range(TILES)], [scaled[t][:] for t in range(TILES)])):
+            for t in range(TILES):
+                for b in range(TURNED):
+                    nc.tensor.matmul(
+                        sums[b][:, t * P : (t + 1) * P],
+                        source[t][:, b * P : (b + 1) * P],
+                        ident[:],
+                        start=(half == 0 and t == 0),
+                        stop=(half == 1 and t == TILES - 1),
+                        is_transpose=True,
+                    )
+        z_t = [keep.tile([P, H], BF16, name=f"z_t{b}") for b in range(TURNED)]
+        for b in range(TURNED):
+            nc.scalar.activation(
+                z_t[b][:].rearrange("p (u m e) -> p u m e", u=2, e=2),
+                sums[b][:].rearrange("p (u e m) -> p u m e", u=2, e=2),
+                COPY,
+                scale=pivot[:, b : b + 1],
+            )
+
         z = {}
 
-        def gather(r):
-            s0, n, fused = ROUNDS[r]
-            cols = pos_sb[:, s0 // 16 : (s0 + n) // 16]
+        def turn_back(g, copy):
+            pairs = banks[g][:].rearrange("p (i u n) -> p i u n", i=2, u=2)
+            for i in range(2):
+                for u in range(2):
+                    nc.tensor.transpose(
+                        pairs[:, i, u, :], z_t[2 * g + i][:].bitcast(F32)[:, u * P : (u + 1) * P], ident[:]
+                    )
+            s0 = LOW + 2 * g * P
+            z[s0] = keep.tile([P, 8 * P], BF16, name=f"z{s0}", align_bytes=64)
+            copy(
+                z[s0][:].bitcast(F32).rearrange("p (i n u) -> p i n u", i=2, u=2),
+                pairs.rearrange("p i u n -> p i n u"),
+            )
+
+        other = {}
+
+        def scale_partner(r):
+            s0, n = ROUNDS[r]
             other[r] = keep.tile([P, TILES, n], F32, name=f"other{r}")
-            if fused:
-                for t in range(TILES):
-                    nc.vector.tensor_tensor(other[r][:, t, :], h[t][:].indirect(cols), mu_sb[:, s0 : s0 + n], MULT)
-            else:
-                partner = keep.tile([P, TILES, n], F32, name=f"partner{r}")
-                for t in range(TILES):
-                    nc.scalar.activation(partner[:, t, :], h[t][:].indirect(cols), COPY)
-                nc.vector.tensor_tensor(
-                    other[r][:], partner[:], mu_sb[:, s0 : s0 + n].unsqueeze(1).broadcast_to([P, TILES, n]), MULT
-                )
+            nc.vector.tensor_tensor(
+                other[r][:], partner[r][:], mu_sb[:, s0 : s0 + n].unsqueeze(1).broadcast_to([P, TILES, n]), MULT
+            )
 
         def mix(r):
-            s0, n, fused = ROUNDS[r]
-            z[r] = keep.tile([P, 4 * n], BF16, name=f"z{r}", align_bytes=64)
+            s0, n = ROUNDS[r]
+            z[s0] = keep.tile([P, 4 * n], BF16, name=f"z{s0}", align_bytes=64)
             nc.vector.tensor_tensor(
-                z[r][:].rearrange("p (c i t) -> p c t i", i=4, t=TILES),
+                z[s0][:].rearrange("p (c i t) -> p c t i", i=4, t=TILES),
                 other[r][:].rearrange("p t (c i) -> p c t i", i=4),
                 own[:, :, s0 : s0 + n].rearrange("p t (c i) -> p c t i", i=4),
                 ADD,
             )
 
-        def second_layer(r):
-            s0, n, fused = ROUNDS[r]
-            z_code = keep.tile([P, n], U32, name=f"z_code{r}", align_bytes=64)
-            z_scale = keep.tile([P, n], U8, name=f"z_scale{r}", align_bytes=64)
-            nc.vector.quantize_mx(z_code[:].bitcast(FP8X4), z_scale[:], z[r][:])
-            acc = banks[r][:, 0:n]
+        def second_layer(s0, n, bank, copy):
+            z_code = keep.tile([P, n], U32, name=f"z_code{s0}", align_bytes=64)
+            z_scale = keep.tile([P, n], U8, name=f"z_scale{s0}", align_bytes=64)
+            nc.vector.quantize_mx(z_code[:].bitcast(FP8X4), z_scale[:], z[s0][:])
+            acc = banks[bank][:, 0:n]
             nc.tensor.matmul_mx(
                 acc,
                 lhsT=w2_code[:].bitcast(FP8X4),
@@ -152,14 +259,20 @@ def tile_picked_mixup_none_p_kernel(
                 start=True,
                 stop=True,
             )
-            res = keep.tile([P, n], F32, name=f"res{r}")
-            nc.scalar.copy(res[:], acc)
+            res = keep.tile([P, n], F32, name=f"res{s0}")
+            copy(res[:], acc)
             nc.sync.dma_start(out[:, s0 : s0 + n], res[:])
 
-        for r in range(len(ROUNDS) + 1):
-            if r < len(ROUNDS):
-                gather(r)
-            if r >= 1:
-                second_layer(r - 1)
-            if r < len(ROUNDS):
-                mix(r)
+        scale_partner(0)
+        scale_partner(1)
+        mix(0)
+        mix(1)
+        second_layer(0, 256, 4, nc.scalar.copy)
+        scale_partner(2)
+        second_layer(256, 128, 6, nc.scalar.copy)
+        mix(2)
+        turn_back(0, nc.vector.tensor_copy)
+        second_layer(384, 128, 3, nc.scalar.copy)
+        turn_back(1, nc.scalar.copy)
+        second_layer(512, 256, 2, nc.scalar.copy)
+        second_layer(768, 256, 5, nc.vector.tensor_copy)

@@ -21,9 +21,12 @@ P = 128
 BANK = 512
 TILES = H // P
 PIECE = 256
-LOW = 512
-TURNED = (S - LOW) // P
-ROUNDS = [(0, 256), (256, 128), (384, 128)]
+BLOCKS = S // P
+DIRECT = 2
+LOW = DIRECT * P
+SUMMED = BLOCKS - DIRECT
+PAIRS = SUMMED // 2
+W1_LOADS = ((0, 2 * P), (2 * P, 3 * P), (3 * P, H))
 
 
 def tile_picked_mixup_none_p_kernel(
@@ -40,10 +43,8 @@ def tile_picked_mixup_none_p_kernel(
         pos_sb = keep.tile([P, S // 16], U16, name="pos_sb")
         scale_table = keep.tile([P, T], U8, name="scale_table", align_bytes=64)
         word_table = shared.tile([P, T], I32, name="word_table", align_bytes=64, offset=10240)
-        w1_raw = keep.tile([P, 4, H], F32, name="w1_raw")
+        w1_raw = [keep.tile([P, 4, c1 - c0], F32, name=f"w1_raw{c0}") for c0, c1 in W1_LOADS]
         w2_raw = keep.tile([P, 4, N], F32, name="w2_raw")
-        lam_sb = keep.tile([P, LOW], F32, name="lam_sb")
-        mu_sb = keep.tile([P, LOW], F32, name="mu_sb")
         share_rows = keep.tile([P, P], F32, name="share_rows")
         ident = keep.tile([P, P], F32, name="ident")
 
@@ -54,59 +55,62 @@ def tile_picked_mixup_none_p_kernel(
         for r, share in enumerate((lam, mu)):
             nc.sync.dma_start(
                 share_rows[P // 2 * r : P // 2 * (r + 1), :],
-                share[0 : P // 2 // TURNED, LOW:S].rearrange("o (b c) -> o b c", c=P),
+                share[0 : P // 2 // BLOCKS, :].rearrange("o (b c) -> o b c", c=P),
             )
         w1_rows = w1.rearrange("(p j) c -> p j c", j=4)
-        nc.sync.dma_start(w1_raw[:, 0:3, :], w1_rows[:, 0:3, :])
+        nc.sync.dma_start(w1_raw[0][:], w1_rows[:, :, slice(*W1_LOADS[0])])
         nc.sync.dma_start(offs_sb[:], offs)
         for q in range(4):
             nc.sync.dma_start(
                 scale_table[32 * q : 32 * q + 4, :].bitcast(I32),
                 x_scales[0][4 * q : 4 * q + 4, :].bitcast(I32),
             )
-        nc.sync.dma_start(w1_raw[:, 3:4, :], w1_rows[:, 3:4, :])
+        nc.sync.dma_start(w1_raw[1][:], w1_rows[:, :, slice(*W1_LOADS[1])])
         nc.sync.dma_start(word_table[:], x_words[0].rearrange("p n t -> p (n t)").bitcast(I32))
-        nc.sync.dma_start(w2_raw[:], w2.rearrange("(p j) n -> p j n", j=4))
-        nc.sync.dma_start(lam_sb[:], lam[:, 0:LOW])
+        nc.sync.dma_start(w1_raw[2][:], w1_rows[:, :, slice(*W1_LOADS[2])])
         nc.sync.dma_start(pos_sb[:], pos1)
-        nc.sync.dma_start(mu_sb[:], mu[:, 0:LOW])
+        nc.sync.dma_start(w2_raw[:], w2.rearrange("(p j) n -> p j n", j=4))
 
-        nc.tensor.transpose(banks[6][:, 0:P], share_rows[:], ident[:])
-        lam_col = banks[6][:, 0:TURNED]
-        mu_col = banks[6][:, P // 2 : P // 2 + TURNED]
+        nc.tensor.transpose(banks[5][:, 0:P], share_rows[:], ident[:])
+        lam_col = banks[5][:, DIRECT:BLOCKS]
+        mu_col = banks[5][:, P // 2 + DIRECT : P // 2 + BLOCKS]
         nudge_tile = shared.tile([P, 32], F32, name="nudge_tile", align_bytes=64, offset=4096 - 64)
-        nudge = nudge_tile[:, 0:TURNED]
-        pivot = keep.tile([P, TURNED], F32, name="pivot")
+        nudge = nudge_tile[:, 0:SUMMED]
+        pivot = keep.tile([P, SUMMED], F32, name="pivot")
         inverse_tile = shared.tile([P, 32], F32, name="inverse_tile", align_bytes=64, offset=7168 - 64)
-        inverse = inverse_tile[:, 0:TURNED]
-        ratio_col = keep.tile([P, TURNED], F32, name="ratio_col")
+        inverse = inverse_tile[:, 0:SUMMED]
+        ratio_col = keep.tile([P, SUMMED], F32, name="ratio_col")
+        direct_shares = keep.tile([P, 2, DIRECT], F32, name="direct_shares")
         nc.scalar.activation(nudge, mu_col, COPY, bias=2.0**-100, scale=2.0**-40)
+        nc.scalar.copy(direct_shares[:], banks[5][:, 0:P].rearrange("p (r c) -> p r c", r=2)[:, :, 0:DIRECT])
         nc.vector.tensor_tensor(pivot[:], lam_col, nudge, ADD)
         nc.vector.reciprocal(inverse, pivot[:])
         nc.vector.tensor_tensor(ratio_col[:], mu_col, inverse, MULT)
-        for b in range(TURNED):
+        for b in range(SUMMED):
             nc.tensor.transpose(
-                banks[7][:, b * P : (b + 1) * P], ratio_col[:, b : b + 1].to_broadcast([P, P]), ident[:]
+                banks[6 + b // 4][:, b % 4 * P : (b % 4 + 1) * P], ratio_col[:, b : b + 1].to_broadcast([P, P]), ident[:]
             )
 
         w1_grouped = [
-            shared.tile([P, 2, P, 4], BF16, name=f"w1_grouped{i}", align_bytes=64, offset=2048 * (i + 1))
+            shared.tile([P, 2, P * 4], BF16, name=f"w1_grouped{i}", align_bytes=64, offset=(2048, 4096)[i])
             for i in range(2)
         ]
-        for i in range(2):
-            nc.scalar.activation(
-                w1_grouped[i][:].rearrange("p t m j -> p m j t"),
-                w1_raw[:].rearrange("p j (m t) -> p m j t", t=TILES)[:, :, :, 2 * i : 2 * i + 2],
-                COPY,
+
+        def cast_w1(t):
+            nc.scalar.copy(
+                w1_grouped[t // 2][:, t % 2, :].rearrange("p (u q e j) -> p q j u e", u=2, e=2, j=4),
+                w1_raw[max(t - 1, 0)][:, :, (t == 1) * P : (t == 1) * P + P].rearrange("p j (q u e) -> p q j u e", u=2, e=2),
             )
-        ratio = keep.tile([P, S - LOW], F32, name="ratio")
-        nc.scalar.copy(ratio[:], banks[7][:])
+
+        cast_w1(0)
+        cast_w1(1)
+        cast_w1(2)
+        ratio = shared.tile([P, S - LOW], F32, name="ratio", align_bytes=64, offset=24576)
+        nc.scalar.copy(ratio[:, 0:BANK], banks[6][:])
+        nc.scalar.copy(ratio[:, BANK : S - LOW], banks[7][:, 0 : S - LOW - BANK])
+        cast_w1(3)
         w2_grouped = keep.tile([P, N * 4], BF16, name="w2_grouped", align_bytes=64)
-        nc.scalar.activation(
-            w2_grouped[:].rearrange("p (c i j) -> p c j i", i=4, j=4),
-            w2_raw[:].rearrange("p j (c i) -> p c j i", i=4),
-            COPY,
-        )
+        nc.gpsimd.tensor_copy(w2_grouped[:].rearrange("p (n j) -> p n j", j=4), w2_raw[:].rearrange("p j n -> p n j"))
 
         x_code = shared.tile([P, S], U32, name="x_code", align_bytes=64, offset=0)
         w1_codes = [
@@ -118,7 +122,7 @@ def tile_picked_mixup_none_p_kernel(
         def quantise_w1(i):
             cols = slice(2 * P * i, 2 * P * (i + 1))
             nc.vector.quantize_mx(
-                w1_codes[i][:].bitcast(FP8X4), w1_scales[:, cols], w1_grouped[i][:].rearrange("p t m j -> p (t m j)")
+                w1_codes[i][:].bitcast(FP8X4), w1_scales[:, cols], w1_grouped[i][:].rearrange("p t c -> p (t c)")
             )
 
         nc.vector.tensor_copy(x_scale[:], scale_table[:].indirect(offs_sb[:]))
@@ -131,34 +135,44 @@ def tile_picked_mixup_none_p_kernel(
         quantise_w1(1)
 
         h = [keep.tile([P, S], F32, name=f"h{t}") for t in range(TILES)]
-        own = keep.tile([P, TILES, LOW], F32, name="own")
-        fills = [((0, 1), t0, PIECE) for t0 in range(0, S, PIECE)]
-        fills = fills + [((t,), t0, BANK) for t in (2, 3) for t0 in (0, BANK)]
 
-        def own_share(i):
-            tiles, t0, n = fills[i]
-            nc.vector.tensor_tensor(
-                own[:, tiles[0] : tiles[-1] + 1, t0 : t0 + n],
-                banks[i][:].rearrange("p (i n) -> p i n", n=n),
-                lam_sb[:, t0 : t0 + n].unsqueeze(1).broadcast_to([P, len(tiles), n]),
-                MULT,
+        def first_layer(i, j):
+            t, t0 = i // 4 * 2 + j, i % 4 * PIECE
+            nc.tensor.matmul_mx(
+                banks[i][:, j * PIECE : (j + 1) * PIECE],
+                lhsT=w1_codes[t // 2][:, j * P : (j + 1) * P].bitcast(FP8X4),
+                lhsT_scale=w1_scales[:, t * P : (t + 1) * P],
+                rhs=x_code[:, t0 : t0 + PIECE].bitcast(FP8X4),
+                rhs_scale=x_scale[:, t0 : t0 + PIECE],
+                start=True,
+                stop=True,
             )
 
-        for i, (tiles, t0, n) in enumerate(fills):
-            for j, t in enumerate(tiles):
+        def empty(i, j):
+            t, t0 = i // 4 * 2 + j, i % 4 * PIECE
+            copy = nc.vector.tensor_copy if i == 2 else nc.scalar.copy
+            copy(h[t][:, t0 : t0 + PIECE], banks[i][:, j * PIECE : (j + 1) * PIECE])
+
+        for i in range(8):
+            if i == 3:
+                for j in range(2):
+                    first_layer(i, j)
+                    empty(i, j)
+            else:
+                for step in (first_layer, empty):
+                    for j in range(2):
+                        step(i, j)
+        for b in range(DIRECT):
+            for i in range(2):
                 nc.tensor.matmul_mx(
-                    banks[i][:, j * n : (j + 1) * n],
-                    lhsT=w1_codes[t // 2][:, t % 2 * P : (t % 2 + 1) * P].bitcast(FP8X4),
-                    lhsT_scale=w1_scales[:, t * P : (t + 1) * P],
-                    rhs=x_code[:, t0 : t0 + n].bitcast(FP8X4),
-                    rhs_scale=x_scale[:, t0 : t0 + n],
+                    banks[6 + b][:, i * PIECE : (i + 1) * PIECE],
+                    lhsT=x_code[:, b * P : (b + 1) * P].bitcast(FP8X4),
+                    lhsT_scale=x_scale[:, b * P : (b + 1) * P],
+                    rhs=w1_codes[i][:].bitcast(FP8X4),
+                    rhs_scale=w1_scales[:, i * PIECE : (i + 1) * PIECE],
                     start=True,
                     stop=True,
                 )
-            for j, t in enumerate(tiles):
-                nc.scalar.copy(h[t][:, t0 : t0 + n], banks[i][:, j * n : (j + 1) * n])
-        own_share(0)
-        own_share(1)
 
         scaled = [keep.tile([P, S - LOW], F32, name=f"scaled{t}") for t in range(TILES)]
 
@@ -170,88 +184,98 @@ def tile_picked_mixup_none_p_kernel(
                 MULT,
             )
 
-        gather_scaled(0, 0, 512)
-        gather_scaled(1, 0, 512)
-        own_share(4)
-        gather_scaled(2, 0, 512)
-        gather_scaled(3, 0, 256)
-        gather_scaled(3, 256, 256)
-        own_share(6)
-        w2_code = keep.tile([P, N], U32, name="w2_code", align_bytes=64)
+        gather_scaled(0, 0, S - LOW)
+        gather_scaled(1, 0, S - LOW)
+        for g in range(PAIRS):
+            for t in (2, 3):
+                gather_scaled(t, g * PIECE, PIECE)
+        w2_code = shared.tile([P, N], U32, name="w2_code", align_bytes=64, offset=14336)
         w2_scale = keep.tile([P, N], U8, name="w2_scale", align_bytes=64)
         nc.vector.quantize_mx(w2_code[:].bitcast(FP8X4), w2_scale[:], w2_grouped[:])
 
-        partner = []
-        for r, (s0, n) in enumerate(ROUNDS):
-            partner.append(
-                shared.tile([P, TILES, n], F32, name=f"partner{r}", align_bytes=64, offset=(0, 10240, 7168)[r])
-            )
-            for t in range(TILES):
-                nc.scalar.activation(partner[r][:, t, :], h[t][:].indirect(pos_sb[:, s0 // 16 : (s0 + n) // 16]), COPY)
+        def in_z_order(bank):
+            return bank[:].rearrange("p (t u m) -> p u t m", t=TILES, u=2)
 
-        sums = [banks[i] for i in (2, 3, 5, 7)]
-        for half, source in enumerate(([h[t][:, LOW:S] for t in range(TILES)], [scaled[t][:] for t in range(TILES)])):
-            for t in range(TILES):
-                for b in range(TURNED):
+        partner = shared.tile([P, TILES, LOW], F32, name="partner", align_bytes=64, offset=0)
+        direct_own = [keep.tile([P, H], F32, name=f"direct_own{b}") for b in range(DIRECT)]
+        for t in range(TILES):
+            nc.scalar.activation(partner[:, t, :], h[t][:].indirect(pos_sb[:, 0 : LOW // 16]), COPY)
+            if t == 1:
+                for b in range(DIRECT):
+                    nc.scalar.activation(
+                        direct_own[b][:].rearrange("p (u t m) -> p u t m", t=TILES, u=2),
+                        in_z_order(banks[6 + b]),
+                        COPY,
+                        scale=direct_shares[:, 0, b : b + 1],
+                    )
+
+        sources = ([h[t][:, LOW:S] for t in range(TILES)], [scaled[t][:] for t in range(TILES)])
+        steps = [(0, 2), (0, 3), (0, 0), (0, 1), (1, 0), (1, 1), (1, 2), (1, 3)]
+
+        def add_turned(g, some):
+            for half, t in some:
+                for b in (2 * g, 2 * g + 1):
                     nc.tensor.matmul(
-                        sums[b][:, t * P : (t + 1) * P],
-                        source[t][:, b * P : (b + 1) * P],
+                        banks[b][:, t * P : (t + 1) * P],
+                        sources[half][t][:, b * P : (b + 1) * P],
                         ident[:],
-                        start=(half == 0 and t == 0),
-                        stop=(half == 1 and t == TILES - 1),
+                        start=(half, t) == steps[0],
+                        stop=(half, t) == steps[-1],
                         is_transpose=True,
                     )
-        z_t = [keep.tile([P, H], BF16, name=f"z_t{b}") for b in range(TURNED)]
-        for b in range(TURNED):
+
+        for some in (steps[0:5], steps[5:6]):
+            for g in range(PAIRS):
+                add_turned(g, some)
+        add_turned(0, steps[6:])
+        add_turned(1, steps[6:])
+        for b in range(DIRECT):
+            for t in range(TILES):
+                nc.tensor.transpose(banks[6 + b][:, t * P : (t + 1) * P], partner[:, t, b * P : (b + 1) * P], ident[:])
+        add_turned(2, steps[6:])
+
+        z_t = [keep.tile([P, H], BF16, name=f"z_t{b}") for b in range(BLOCKS)]
+        for b in range(SUMMED):
             nc.scalar.activation(
-                z_t[b][:].rearrange("p (u m e) -> p u m e", u=2, e=2),
-                sums[b][:].rearrange("p (u e m) -> p u m e", u=2, e=2),
+                z_t[DIRECT + b][:].rearrange("p (u t m) -> p u t m", t=TILES, u=2),
+                in_z_order(banks[b]),
                 COPY,
                 scale=pivot[:, b : b + 1],
             )
+        for b in range(DIRECT):
+            for u in range(2):
+                half = slice(u * 2 * P, (u + 1) * 2 * P)
+                nc.vector.scalar_tensor_tensor(
+                    z_t[b][:, half].rearrange("p (t m) -> p t m", t=TILES),
+                    in_z_order(banks[6 + b])[:, u],
+                    direct_shares[:, 1, b : b + 1],
+                    direct_own[b][:, half].rearrange("p (t m) -> p t m", t=TILES),
+                    MULT,
+                    ADD,
+                )
 
         z = {}
 
-        def turn_back(g, copy):
-            pairs = banks[g][:].rearrange("p (i u n) -> p i u n", i=2, u=2)
-            for i in range(2):
+        def turn_back(b0, nb, bank, copy):
+            pairs = banks[bank][:, 0 : nb * 2 * P].rearrange("p (i u n) -> p i u n", i=nb, u=2)
+            for i in range(nb):
                 for u in range(2):
                     nc.tensor.transpose(
-                        pairs[:, i, u, :], z_t[2 * g + i][:].bitcast(F32)[:, u * P : (u + 1) * P], ident[:]
+                        pairs[:, i, u, :], z_t[b0 + i][:].bitcast(F32)[:, u * P : (u + 1) * P], ident[:]
                     )
-            s0 = LOW + 2 * g * P
-            z[s0] = keep.tile([P, 8 * P], BF16, name=f"z{s0}", align_bytes=64)
+            z[b0] = shared.tile([P, 4 * nb * P], BF16, name=f"z{b0}", align_bytes=64, offset=28672 + 1024 * b0)
             copy(
-                z[s0][:].bitcast(F32).rearrange("p (i n u) -> p i n u", i=2, u=2),
-                pairs.rearrange("p i u n -> p i n u"),
+                z[b0][:].bitcast(F32).rearrange("p (i c j u) -> p i c u j", i=nb, j=2, u=2),
+                pairs.rearrange("p i u (c j) -> p i c u j", j=2),
             )
 
-        other = {}
-
-        def scale_partner(r):
-            s0, n = ROUNDS[r]
-            other[r] = keep.tile([P, TILES, n], F32, name=f"other{r}")
-            nc.vector.tensor_tensor(
-                other[r][:], partner[r][:], mu_sb[:, s0 : s0 + n].unsqueeze(1).broadcast_to([P, TILES, n]), MULT
-            )
-
-        def mix(r):
-            s0, n = ROUNDS[r]
-            z[s0] = keep.tile([P, 4 * n], BF16, name=f"z{s0}", align_bytes=64)
-            nc.vector.tensor_tensor(
-                z[s0][:].rearrange("p (c i t) -> p c t i", i=4, t=TILES),
-                other[r][:].rearrange("p t (c i) -> p c t i", i=4),
-                own[:, :, s0 : s0 + n].rearrange("p t (c i) -> p c t i", i=4),
-                ADD,
-            )
-
-        def second_layer(s0, n, bank, copy):
-            z_code = keep.tile([P, n], U32, name=f"z_code{s0}", align_bytes=64)
-            z_scale = keep.tile([P, n], U8, name=f"z_scale{s0}", align_bytes=64)
-            nc.vector.quantize_mx(z_code[:].bitcast(FP8X4), z_scale[:], z[s0][:])
-            acc = banks[bank][:, 0:n]
+        def second_layer(b0, nb, bank):
+            n = nb * P
+            z_code = keep.tile([P, n], U32, name=f"z_code{b0}", align_bytes=64)
+            z_scale = keep.tile([P, n], U8, name=f"z_scale{b0}", align_bytes=64)
+            nc.vector.quantize_mx(z_code[:].bitcast(FP8X4), z_scale[:], z[b0][:])
             nc.tensor.matmul_mx(
-                acc,
+                banks[bank][:, 0:n],
                 lhsT=w2_code[:].bitcast(FP8X4),
                 lhsT_scale=w2_scale[:],
                 rhs=z_code[:].bitcast(FP8X4),
@@ -259,20 +283,23 @@ def tile_picked_mixup_none_p_kernel(
                 start=True,
                 stop=True,
             )
-            res = keep.tile([P, n], F32, name=f"res{s0}")
-            copy(res[:], acc)
-            nc.sync.dma_start(out[:, s0 : s0 + n], res[:])
 
-        scale_partner(0)
-        scale_partner(1)
-        mix(0)
-        mix(1)
-        second_layer(0, 256, 4, nc.scalar.copy)
-        scale_partner(2)
-        second_layer(256, 128, 6, nc.scalar.copy)
-        mix(2)
-        turn_back(0, nc.vector.tensor_copy)
-        second_layer(384, 128, 3, nc.scalar.copy)
-        turn_back(1, nc.scalar.copy)
-        second_layer(512, 256, 2, nc.scalar.copy)
-        second_layer(768, 256, 5, nc.vector.tensor_copy)
+        def store(b0, nb, bank, copy, offset):
+            n = nb * P
+            res = shared.tile([P, n], F32, name=f"res{b0}", align_bytes=64, offset=offset)
+            copy(res[:], banks[bank][:, 0:n])
+            nc.sync.dma_start(out[:, b0 * P : b0 * P + n], res[:])
+
+        turn_back(2, 2, 0, nc.vector.tensor_copy)
+        turn_back(0, 2, 1, nc.vector.tensor_copy)
+        turn_back(4, 2, 2, nc.scalar.copy)
+        turn_back(6, 1, 4, nc.scalar.copy)
+        turn_back(7, 1, 3, nc.scalar.copy)
+        groups = [(2, 2, 6), (0, 2, 7), (4, 2, 0), (6, 1, 5), (7, 1, 1)]
+        for group in groups:
+            second_layer(*group)
+        store(*groups[0], nc.scalar.copy, 36864)
+        store(*groups[1], nc.scalar.copy, 37888)
+        store(*groups[2], nc.vector.tensor_copy, 35840)
+        store(*groups[3], nc.scalar.copy, 38912)
+        store(*groups[4], nc.scalar.copy, 39936)

@@ -45,7 +45,7 @@ def tile_picked_mixup_none_p_kernel(
         word_table = shared.tile([P, T], I32, name="word_table", align_bytes=64, offset=10240)
         w1_raw = [keep.tile([P, 4, c1 - c0], F32, name=f"w1_raw{c0}") for c0, c1 in W1_LOADS]
         w2_raw = keep.tile([P, 4, N], F32, name="w2_raw")
-        share_rows = keep.tile([P, P], F32, name="share_rows")
+        share_rows = shared.tile([P, P], F32, name="share_rows", align_bytes=64, offset=2048)
         ident = keep.tile([P, P], F32, name="ident")
 
         nc.vector.memset(scale_table[:, 0 : T // 2].bitcast(I32), 0)
@@ -65,58 +65,65 @@ def tile_picked_mixup_none_p_kernel(
                 scale_table[32 * q : 32 * q + 4, :].bitcast(I32),
                 x_scales[0][4 * q : 4 * q + 4, :].bitcast(I32),
             )
-        nc.sync.dma_start(w1_raw[1][:], w1_rows[:, :, slice(*W1_LOADS[1])])
         nc.sync.dma_start(word_table[:], x_words[0].rearrange("p n t -> p (n t)").bitcast(I32))
+        nc.sync.dma_start(w1_raw[1][:], w1_rows[:, :, slice(*W1_LOADS[1])])
         nc.sync.dma_start(w1_raw[2][:], w1_rows[:, :, slice(*W1_LOADS[2])])
         nc.sync.dma_start(pos_sb[:], pos1)
         nc.sync.dma_start(w2_raw[:], w2.rearrange("(p j) n -> p j n", j=4))
 
         nc.tensor.transpose(banks[5][:, 0:P], share_rows[:], ident[:])
-        lam_col = banks[5][:, DIRECT:BLOCKS]
-        mu_col = banks[5][:, P // 2 + DIRECT : P // 2 + BLOCKS]
-        nudge_tile = shared.tile([P, 32], F32, name="nudge_tile", align_bytes=64, offset=4096 - 64)
+        shares = keep.tile([P, 2, BLOCKS], F32, name="shares")
+        nc.scalar.activation(shares[:], banks[5][:, 0:P].rearrange("p (r c) -> p r c", r=2)[:, :, 0:BLOCKS], COPY)
+        lam_col = shares[:, 0, DIRECT:BLOCKS]
+        mu_col = shares[:, 1, DIRECT:BLOCKS]
+        nudge_tile = shared.tile([P, 32], F32, name="nudge_tile", align_bytes=64, offset=7168 - 64)
         nudge = nudge_tile[:, 0:SUMMED]
         pivot = keep.tile([P, SUMMED], F32, name="pivot")
-        inverse_tile = shared.tile([P, 32], F32, name="inverse_tile", align_bytes=64, offset=7168 - 64)
-        inverse = inverse_tile[:, 0:SUMMED]
-        ratio_col = keep.tile([P, SUMMED], F32, name="ratio_col")
-        direct_shares = keep.tile([P, 2, DIRECT], F32, name="direct_shares")
-        nc.scalar.activation(nudge, mu_col, COPY, bias=2.0**-100, scale=2.0**-40)
-        nc.scalar.copy(direct_shares[:], banks[5][:, 0:P].rearrange("p (r c) -> p r c", r=2)[:, :, 0:DIRECT])
-        nc.vector.tensor_tensor(pivot[:], lam_col, nudge, ADD)
-        nc.vector.reciprocal(inverse, pivot[:])
-        nc.vector.tensor_tensor(ratio_col[:], mu_col, inverse, MULT)
+        inverse = keep.tile([P, SUMMED], F32, name="inverse")
+        ratio_tile = shared.tile([P, 32], F32, name="ratio_tile", align_bytes=64, offset=20480 - 64)
+        ratio_col = ratio_tile[:, 0:SUMMED]
+        nc.gpsimd.tensor_scalar(nudge, mu_col, 2.0**-40, 2.0**-100, MULT, ADD)
+        nc.gpsimd.tensor_tensor(pivot[:], lam_col, nudge, ADD)
+        nc.vector.reciprocal(inverse[:], pivot[:])
+        nc.gpsimd.tensor_tensor(ratio_col, mu_col, inverse[:], MULT)
         for b in range(SUMMED):
             nc.tensor.transpose(
                 banks[6 + b // 4][:, b % 4 * P : (b % 4 + 1) * P], ratio_col[:, b : b + 1].to_broadcast([P, P]), ident[:]
             )
 
-        w1_grouped = [
-            shared.tile([P, 2, P * 4], BF16, name=f"w1_grouped{i}", align_bytes=64, offset=(2048, 4096)[i])
-            for i in range(2)
-        ]
+        low_grouped = shared.tile([P, 2, P * 4], BF16, name="low_grouped", align_bytes=64, offset=2048)
+        high_grouped = shared.tile([P, 2, P * 4], BF16, name="high_grouped", align_bytes=64, offset=20480)
+        w1_grouped = [low_grouped, high_grouped]
 
-        def cast_w1(t):
-            nc.scalar.copy(
-                w1_grouped[t // 2][:, t % 2, :].rearrange("p (u q e j) -> p q j u e", u=2, e=2, j=4),
-                w1_raw[max(t - 1, 0)][:, :, (t == 1) * P : (t == 1) * P + P].rearrange("p j (q u e) -> p q j u e", u=2, e=2),
+        def cast_views(t, order):
+            return (
+                w1_grouped[t // 2][:, t % 2, :].rearrange("p (u q e j) -> p " + order, u=2, e=2, j=4),
+                w1_raw[max(t - 1, 0)][:, :, (t == 1) * P : (t == 1) * P + P].rearrange(
+                    "p j (q u e) -> p " + order, u=2, e=2
+                ),
             )
 
-        cast_w1(0)
-        cast_w1(1)
-        cast_w1(2)
+        nc.scalar.copy(*cast_views(0, "q j u e"))
+        nc.scalar.copy(*cast_views(1, "q j u e"))
         ratio = shared.tile([P, S - LOW], F32, name="ratio", align_bytes=64, offset=24576)
         nc.scalar.copy(ratio[:, 0:BANK], banks[6][:])
         nc.scalar.copy(ratio[:, BANK : S - LOW], banks[7][:, 0 : S - LOW - BANK])
-        cast_w1(3)
-        w2_grouped = keep.tile([P, N * 4], BF16, name="w2_grouped", align_bytes=64)
+        nc.gpsimd.tensor_copy(*cast_views(2, "q u e j"))
+        nc.scalar.copy(*cast_views(3, "q j u e"))
+        w2_grouped = shared.tile([P, N * 4], BF16, name="w2_grouped", align_bytes=64, offset=19456)
         nc.gpsimd.tensor_copy(w2_grouped[:].rearrange("p (n j) -> p n j", j=4), w2_raw[:].rearrange("p j n -> p n j"))
 
         x_code = shared.tile([P, S], U32, name="x_code", align_bytes=64, offset=0)
         w1_codes = [
             shared.tile([P, 2 * P], U32, name=f"w1_codes{i}", align_bytes=64, offset=(6144, 10240)[i]) for i in range(2)
         ]
-        x_scale = shared.tile([P, S], U8, name="x_scale", align_bytes=64, offset=7168)
+        x_scale_halves = [
+            shared.tile([P, BANK], U8, name=f"x_scale{i}", align_bytes=64, offset=(7680, 7168)[i]) for i in range(2)
+        ]
+
+        def x_scale(t0, n):
+            return x_scale_halves[t0 // BANK][:, t0 % BANK : t0 % BANK + n]
+
         w1_scales = keep.tile([P, H], U8, name="w1_scales", align_bytes=64)
 
         def quantise_w1(i):
@@ -125,7 +132,10 @@ def tile_picked_mixup_none_p_kernel(
                 w1_codes[i][:].bitcast(FP8X4), w1_scales[:, cols], w1_grouped[i][:].rearrange("p t c -> p (t c)")
             )
 
-        nc.vector.tensor_copy(x_scale[:], scale_table[:].indirect(offs_sb[:]))
+        for i in range(2):
+            nc.vector.tensor_copy(
+                x_scale_halves[i][:], scale_table[:].indirect(offs_sb[:, i * BANK // 16 : (i + 1) * BANK // 16])
+            )
         quantise_w1(0)
         for t0 in range(0, S, PIECE):
             nc.vector.tensor_copy(
@@ -143,7 +153,7 @@ def tile_picked_mixup_none_p_kernel(
                 lhsT=w1_codes[t // 2][:, j * P : (j + 1) * P].bitcast(FP8X4),
                 lhsT_scale=w1_scales[:, t * P : (t + 1) * P],
                 rhs=x_code[:, t0 : t0 + PIECE].bitcast(FP8X4),
-                rhs_scale=x_scale[:, t0 : t0 + PIECE],
+                rhs_scale=x_scale(t0, PIECE),
                 start=True,
                 stop=True,
             )
@@ -167,7 +177,7 @@ def tile_picked_mixup_none_p_kernel(
                 nc.tensor.matmul_mx(
                     banks[6 + b][:, i * PIECE : (i + 1) * PIECE],
                     lhsT=x_code[:, b * P : (b + 1) * P].bitcast(FP8X4),
-                    lhsT_scale=x_scale[:, b * P : (b + 1) * P],
+                    lhsT_scale=x_scale(b * P, P),
                     rhs=w1_codes[i][:].bitcast(FP8X4),
                     rhs_scale=w1_scales[:, i * PIECE : (i + 1) * PIECE],
                     start=True,
@@ -206,7 +216,7 @@ def tile_picked_mixup_none_p_kernel(
                         direct_own[b][:].rearrange("p (u t m) -> p u t m", t=TILES, u=2),
                         in_z_order(banks[6 + b]),
                         COPY,
-                        scale=direct_shares[:, 0, b : b + 1],
+                        scale=shares[:, 0, b : b + 1],
                     )
 
         sources = ([h[t][:, LOW:S] for t in range(TILES)], [scaled[t][:] for t in range(TILES)])
@@ -248,7 +258,7 @@ def tile_picked_mixup_none_p_kernel(
                 nc.vector.scalar_tensor_tensor(
                     z_t[b][:, half].rearrange("p (t m) -> p t m", t=TILES),
                     in_z_order(banks[6 + b])[:, u],
-                    direct_shares[:, 1, b : b + 1],
+                    shares[:, 1, b : b + 1],
                     direct_own[b][:, half].rearrange("p (t m) -> p t m", t=TILES),
                     MULT,
                     ADD,

@@ -26,7 +26,6 @@ DIRECT = 2
 LOW = DIRECT * P
 SUMMED = BLOCKS - DIRECT
 PAIRS = SUMMED // 2
-W1_LOADS = ((0, 2 * P), (2 * P, 3 * P), (3 * P, H))
 
 
 def tile_picked_mixup_none_p_kernel(
@@ -43,7 +42,7 @@ def tile_picked_mixup_none_p_kernel(
         pos_sb = keep.tile([P, S // 16], U16, name="pos_sb")
         scale_table = keep.tile([P, T], U8, name="scale_table", align_bytes=64)
         word_table = shared.tile([P, T], I32, name="word_table", align_bytes=64, offset=10240)
-        w1_raw = [keep.tile([P, 4, c1 - c0], F32, name=f"w1_raw{c0}") for c0, c1 in W1_LOADS]
+        w1_raw = [keep.tile([P, 4, H // 2], F32, name=f"w1_raw{i}") for i in range(2)]
         w2_raw = keep.tile([P, 4, N], F32, name="w2_raw")
         share_rows = shared.tile([P, P], F32, name="share_rows", align_bytes=64, offset=2048)
         ident = keep.tile([P, P], F32, name="ident")
@@ -58,7 +57,7 @@ def tile_picked_mixup_none_p_kernel(
                 share[0 : P // 2 // BLOCKS, :].rearrange("o (b c) -> o b c", c=P),
             )
         w1_rows = w1.rearrange("(p j) c -> p j c", j=4)
-        nc.sync.dma_start(w1_raw[0][:], w1_rows[:, :, slice(*W1_LOADS[0])])
+        nc.sync.dma_start(w1_raw[0][:], w1_rows[:, :, 0 : H // 2])
         nc.sync.dma_start(offs_sb[:], offs)
         for q in range(4):
             nc.sync.dma_start(
@@ -66,8 +65,7 @@ def tile_picked_mixup_none_p_kernel(
                 x_scales[0][4 * q : 4 * q + 4, :].bitcast(I32),
             )
         nc.sync.dma_start(word_table[:], x_words[0].rearrange("p n t -> p (n t)").bitcast(I32))
-        nc.sync.dma_start(w1_raw[1][:], w1_rows[:, :, slice(*W1_LOADS[1])])
-        nc.sync.dma_start(w1_raw[2][:], w1_rows[:, :, slice(*W1_LOADS[2])])
+        nc.sync.dma_start(w1_raw[1][:], w1_rows[:, :, H // 2 : H])
         nc.sync.dma_start(pos_sb[:], pos1)
         nc.sync.dma_start(w2_raw[:], w2.rearrange("(p j) n -> p j n", j=4))
 
@@ -80,12 +78,11 @@ def tile_picked_mixup_none_p_kernel(
         nudge = nudge_tile[:, 0:SUMMED]
         pivot = keep.tile([P, SUMMED], F32, name="pivot")
         inverse = keep.tile([P, SUMMED], F32, name="inverse")
-        ratio_tile = shared.tile([P, 32], F32, name="ratio_tile", align_bytes=64, offset=20480 - 64)
-        ratio_col = ratio_tile[:, 0:SUMMED]
+        ratio_col = shared.tile([P, SUMMED], F32, name="ratio_col", align_bytes=64, offset=20480)
         nc.gpsimd.tensor_scalar(nudge, mu_col, 2.0**-40, 2.0**-100, MULT, ADD)
         nc.gpsimd.tensor_tensor(pivot[:], lam_col, nudge, ADD)
         nc.vector.reciprocal(inverse[:], pivot[:])
-        nc.gpsimd.tensor_tensor(ratio_col, mu_col, inverse[:], MULT)
+        nc.gpsimd.tensor_tensor(ratio_col[:], mu_col, inverse[:], MULT)
         for b in range(SUMMED):
             nc.tensor.transpose(
                 banks[6 + b // 4][:, b % 4 * P : (b % 4 + 1) * P], ratio_col[:, b : b + 1].to_broadcast([P, P]), ident[:]
@@ -98,7 +95,7 @@ def tile_picked_mixup_none_p_kernel(
         def cast_views(t, order):
             return (
                 w1_grouped[t // 2][:, t % 2, :].rearrange("p (u q e j) -> p " + order, u=2, e=2, j=4),
-                w1_raw[max(t - 1, 0)][:, :, (t == 1) * P : (t == 1) * P + P].rearrange(
+                w1_raw[t // 2][:, :, t % 2 * P : (t % 2 + 1) * P].rearrange(
                     "p j (q u e) -> p " + order, u=2, e=2
                 ),
             )
@@ -110,8 +107,6 @@ def tile_picked_mixup_none_p_kernel(
         nc.scalar.copy(ratio[:, BANK : S - LOW], banks[7][:, 0 : S - LOW - BANK])
         nc.gpsimd.tensor_copy(*cast_views(2, "q u e j"))
         nc.scalar.copy(*cast_views(3, "q j u e"))
-        w2_grouped = shared.tile([P, N * 4], BF16, name="w2_grouped", align_bytes=64, offset=19456)
-        nc.gpsimd.tensor_copy(w2_grouped[:].rearrange("p (n j) -> p n j", j=4), w2_raw[:].rearrange("p j n -> p n j"))
 
         x_code = shared.tile([P, S], U32, name="x_code", align_bytes=64, offset=0)
         w1_codes = [
@@ -199,17 +194,18 @@ def tile_picked_mixup_none_p_kernel(
         for g in range(PAIRS):
             for t in (2, 3):
                 gather_scaled(t, g * PIECE, PIECE)
-        w2_code = shared.tile([P, N], U32, name="w2_code", align_bytes=64, offset=14336)
-        w2_scale = keep.tile([P, N], U8, name="w2_scale", align_bytes=64)
-        nc.vector.quantize_mx(w2_code[:].bitcast(FP8X4), w2_scale[:], w2_grouped[:])
+        w2_grouped = shared.tile([P, N * 4], BF16, name="w2_grouped", align_bytes=64, offset=24576)
+        nc.gpsimd.tensor_copy(w2_grouped[:].rearrange("p (n j) -> p n j", j=4), w2_raw[:].rearrange("p j n -> p n j"))
 
         def in_z_order(bank):
             return bank[:].rearrange("p (t u m) -> p u t m", t=TILES, u=2)
 
-        partner = shared.tile([P, TILES, LOW], F32, name="partner", align_bytes=64, offset=0)
-        direct_own = [keep.tile([P, H], F32, name=f"direct_own{b}") for b in range(DIRECT)]
+        partner = [keep.tile([P, LOW], F32, name=f"partner{t}") for t in range(TILES)]
+        direct_own = [
+            shared.tile([P, H], F32, name=f"direct_own{b}", align_bytes=64, offset=40960 + 2048 * b) for b in range(DIRECT)
+        ]
         for t in range(TILES):
-            nc.scalar.activation(partner[:, t, :], h[t][:].indirect(pos_sb[:, 0 : LOW // 16]), COPY)
+            nc.scalar.activation(partner[t][:], h[t][:].indirect(pos_sb[:, 0 : LOW // 16]), COPY)
             if t == 1:
                 for b in range(DIRECT):
                     nc.scalar.activation(
@@ -241,7 +237,11 @@ def tile_picked_mixup_none_p_kernel(
         add_turned(1, steps[6:])
         for b in range(DIRECT):
             for t in range(TILES):
-                nc.tensor.transpose(banks[6 + b][:, t * P : (t + 1) * P], partner[:, t, b * P : (b + 1) * P], ident[:])
+                nc.tensor.transpose(
+                    banks[6 + b][:].rearrange("p (u t m) -> p t u m", t=TILES, u=2)[:, t],
+                    partner[t][:, b * P : (b + 1) * P],
+                    ident[:],
+                )
         add_turned(2, steps[6:])
 
         z_t = [keep.tile([P, H], BF16, name=f"z_t{b}") for b in range(BLOCKS)]
@@ -253,16 +253,13 @@ def tile_picked_mixup_none_p_kernel(
                 scale=pivot[:, b : b + 1],
             )
         for b in range(DIRECT):
-            for u in range(2):
-                half = slice(u * 2 * P, (u + 1) * 2 * P)
-                nc.vector.scalar_tensor_tensor(
-                    z_t[b][:, half].rearrange("p (t m) -> p t m", t=TILES),
-                    in_z_order(banks[6 + b])[:, u],
-                    shares[:, 1, b : b + 1],
-                    direct_own[b][:, half].rearrange("p (t m) -> p t m", t=TILES),
-                    MULT,
-                    ADD,
-                )
+            nc.vector.scalar_tensor_tensor(
+                z_t[b][:], banks[6 + b][:], shares[:, 1, b : b + 1], direct_own[b][:], MULT, ADD
+            )
+
+        w2_code = shared.tile([P, N], U32, name="w2_code", align_bytes=64, offset=40960)
+        w2_scale = keep.tile([P, N], U8, name="w2_scale", align_bytes=64)
+        nc.vector.quantize_mx(w2_code[:].bitcast(FP8X4), w2_scale[:], w2_grouped[:])
 
         z = {}
 

from contextlib import ExitStack

import concourse.mybir as mybir
from concourse.masks import make_identity

K, T, S, H, N = 512, 2048, 1024, 512, 128
FLOPS = 2 * K * H * S + 2 * H * N * S

F32 = mybir.dt.float32
BF16 = mybir.dt.bfloat16
I32 = mybir.dt.int32
U32 = mybir.dt.uint32
U16 = mybir.dt.uint16
U8 = mybir.dt.uint8
FP8X4 = mybir.dt.float8_e4m3fn_x4
COPY = mybir.ActivationFunctionType.Copy
MULT = mybir.AluOpType.mult
ADD = mybir.AluOpType.add

P = 128
BANK = 512
TILES = H // P
PIECE = 256
BLOCKS = S // P
DIRECT = 2
LOW = DIRECT * P
SUMMED = BLOCKS - DIRECT
PAIRS = SUMMED // 2


def tile_picked_mixup_none_p_kernel(
    tc, x_words, x_scales, w1, w2, lam, mu, offs, pos1, out
):
    nc = tc.nc
    with ExitStack() as ctx:
        keep = ctx.enter_context(tc.tile_pool(name="keep", bufs=1))
        shared = ctx.enter_context(tc.tile_pool(name="shared", bufs=1))
        psum = ctx.enter_context(tc.psum_pool(name="psum", bufs=1))
        banks = [psum.tile([P, BANK], F32, name=f"bank{i}") for i in range(8)]

        offs_sb = keep.tile([P, S // 16], U16, name="offs_sb")
        pos_sb = keep.tile([P, S // 16], U16, name="pos_sb")
        scale_table = keep.tile([P, T], U8, name="scale_table", align_bytes=64)
        word_table = shared.tile([P, T], I32, name="word_table", align_bytes=64, offset=10240)
        w1_raw = [keep.tile([P, 4, H // 2], F32, name=f"w1_raw{i}") for i in range(2)]
        w2_raw = keep.tile([P, 4, N], F32, name="w2_raw")
        share_rows = shared.tile([P, P], F32, name="share_rows", align_bytes=64, offset=2048)
        ident = keep.tile([P, P], F32, name="ident")

        nc.vector.memset(scale_table[:, 0 : T // 2].bitcast(I32), 0)
        nc.gpsimd.memset(scale_table[:, T // 2 : T].bitcast(I32), 0)
        make_identity(nc, ident[:])

        for r, share in enumerate((lam, mu)):
            nc.sync.dma_start(
                share_rows[P // 2 * r : P // 2 * (r + 1), :],
                share[0 : P // 2 // BLOCKS, :].rearrange("o (b c) -> o b c", c=P),
            )
        w1_rows = w1.rearrange("(p j) c -> p j c", j=4)
        nc.sync.dma_start(w1_raw[0][:], w1_rows[:, :, 0 : H // 2])
        nc.sync.dma_start(offs_sb[:], offs)
        for q in range(4):
            nc.sync.dma_start(
                scale_table[32 * q : 32 * q + 4, :].bitcast(I32),
                x_scales[0][4 * q : 4 * q + 4, :].bitcast(I32),
            )
        nc.sync.dma_start(word_table[:], x_words[0].rearrange("p n t -> p (n t)").bitcast(I32))
        nc.sync.dma_start(w1_raw[1][:], w1_rows[:, :, H // 2 : H])
        nc.sync.dma_start(pos_sb[:], pos1)
        nc.sync.dma_start(w2_raw[:], w2.rearrange("(p j) n -> p j n", j=4))

        nc.tensor.transpose(banks[5][:, 0:P], share_rows[:], ident[:])
        shares = keep.tile([P, 2, BLOCKS], F32, name="shares")
        nc.scalar.activation(shares[:], banks[5][:, 0:P].rearrange("p (r c) -> p r c", r=2)[:, :, 0:BLOCKS], COPY)
        lam_col = shares[:, 0, DIRECT:BLOCKS]
        mu_col = shares[:, 1, DIRECT:BLOCKS]
        nudge_tile = shared.tile([P, 32], F32, name="nudge_tile", align_bytes=64, offset=7168 - 64)
        nudge = nudge_tile[:, 0:SUMMED]
        pivot = keep.tile([P, SUMMED], F32, name="pivot")
        inverse = keep.tile([P, SUMMED], F32, name="inverse")
        ratio_col = shared.tile([P, SUMMED], F32, name="ratio_col", align_bytes=64, offset=20480)
        nc.gpsimd.tensor_scalar(nudge, mu_col, 2.0**-40, 2.0**-100, MULT, ADD)
        nc.gpsimd.tensor_tensor(pivot[:], lam_col, nudge, ADD)
        nc.vector.reciprocal(inverse[:], pivot[:])
        nc.gpsimd.tensor_tensor(ratio_col[:], mu_col, inverse[:], MULT)
        for b in range(SUMMED):
            nc.tensor.transpose(
                banks[6 + b // 4][:, b % 4 * P : (b % 4 + 1) * P], ratio_col[:, b : b + 1].to_broadcast([P, P]), ident[:]
            )

        low_grouped = shared.tile([P, 2, P * 4], BF16, name="low_grouped", align_bytes=64, offset=2048)
        high_grouped = shared.tile([P, 2, P * 4], BF16, name="high_grouped", align_bytes=64, offset=20480)
        w1_grouped = [low_grouped, high_grouped]

        def cast_views(t, order):
            return (
                w1_grouped[t // 2][:, t % 2, :].rearrange("p (u q e j) -> p " + order, u=2, e=2, j=4),
                w1_raw[t // 2][:, :, t % 2 * P : (t % 2 + 1) * P].rearrange(
                    "p j (q u e) -> p " + order, u=2, e=2
                ),
            )

        nc.scalar.copy(*cast_views(0, "q j u e"))
        nc.scalar.copy(*cast_views(1, "q j u e"))
        ratio = shared.tile([P, S - LOW], F32, name="ratio", align_bytes=64, offset=24576)
        nc.scalar.copy(ratio[:, 0:BANK], banks[6][:])
        nc.scalar.copy(ratio[:, BANK : S - LOW], banks[7][:, 0 : S - LOW - BANK])
        nc.gpsimd.tensor_copy(*cast_views(2, "q u e j"))
        nc.scalar.copy(*cast_views(3, "q j u e"))

        x_code = shared.tile([P, S], U32, name="x_code", align_bytes=64, offset=0)
        w1_codes = [
            shared.tile([P, 2 * P], U32, name=f"w1_codes{i}", align_bytes=64, offset=(6144, 10240)[i]) for i in range(2)
        ]
        x_scale_halves = [
            shared.tile([P, BANK], U8, name=f"x_scale{i}", align_bytes=64, offset=(7680, 7168)[i]) for i in range(2)
        ]

        def x_scale(t0, n):
            return x_scale_halves[t0 // BANK][:, t0 % BANK : t0 % BANK + n]

        w1_scales = keep.tile([P, H], U8, name="w1_scales", align_bytes=64)

        def quantise_w1(i):
            cols = slice(2 * P * i, 2 * P * (i + 1))
            nc.vector.quantize_mx(
                w1_codes[i][:].bitcast(FP8X4), w1_scales[:, cols], w1_grouped[i][:].rearrange("p t c -> p (t c)")
            )

        for i in range(2):
            nc.vector.tensor_copy(
                x_scale_halves[i][:], scale_table[:].indirect(offs_sb[:, i * BANK // 16 : (i + 1) * BANK // 16])
            )
        quantise_w1(0)
        for t0 in range(0, S, PIECE):
            nc.vector.tensor_copy(
                x_code[:, t0 : t0 + PIECE],
                word_table[:].bitcast(U32).indirect(offs_sb[:, t0 // 16 : (t0 + PIECE) // 16]),
            )
        quantise_w1(1)

        h = [keep.tile([P, S], F32, name=f"h{t}") for t in range(TILES)]

        def first_layer(i, j):
            t, t0 = i // 4 * 2 + j, i % 4 * PIECE
            nc.tensor.matmul_mx(
                banks[i][:, j * PIECE : (j + 1) * PIECE],
                lhsT=w1_codes[t // 2][:, j * P : (j + 1) * P].bitcast(FP8X4),
                lhsT_scale=w1_scales[:, t * P : (t + 1) * P],
                rhs=x_code[:, t0 : t0 + PIECE].bitcast(FP8X4),
                rhs_scale=x_scale(t0, PIECE),
                start=True,
                stop=True,
            )

        def empty(i, j):
            t, t0 = i // 4 * 2 + j, i % 4 * PIECE
            copy = nc.vector.tensor_copy if i == 2 else nc.scalar.copy
            copy(h[t][:, t0 : t0 + PIECE], banks[i][:, j * PIECE : (j + 1) * PIECE])

        for i in range(8):
            if i == 3:
                for j in range(2):
                    first_layer(i, j)
                    empty(i, j)
            else:
                for step in (first_layer, empty):
                    for j in range(2):
                        step(i, j)
        for b in range(DIRECT):
            for i in range(2):
                nc.tensor.matmul_mx(
                    banks[6 + b][:, i * PIECE : (i + 1) * PIECE],
                    lhsT=x_code[:, b * P : (b + 1) * P].bitcast(FP8X4),
                    lhsT_scale=x_scale(b * P, P),
                    rhs=w1_codes[i][:].bitcast(FP8X4),
                    rhs_scale=w1_scales[:, i * PIECE : (i + 1) * PIECE],
                    start=True,
                    stop=True,
                )

        scaled = [keep.tile([P, S - LOW], F32, name=f"scaled{t}") for t in range(TILES)]

        def gather_scaled(t, c0, n):
            nc.vector.tensor_tensor(
                scaled[t][:, c0 : c0 + n],
                h[t][:].indirect(pos_sb[:, (LOW + c0) // 16 : (LOW + c0 + n) // 16]),
                ratio[:, c0 : c0 + n],
                MULT,
            )

        gather_scaled(0, 0, S - LOW)
        gather_scaled(1, 0, S - LOW)
        for g in range(PAIRS):
            for t in (2, 3):
                gather_scaled(t, g * PIECE, PIECE)
        w2_grouped = shared.tile([P, N * 4], BF16, name="w2_grouped", align_bytes=64, offset=24576)
        nc.gpsimd.tensor_copy(w2_grouped[:].rearrange("p (n j) -> p n j", j=4), w2_raw[:].rearrange("p j n -> p n j"))

        def in_z_order(bank):
            return bank[:].rearrange("p (t u m) -> p u t m", t=TILES, u=2)

        partner = [keep.tile([P, LOW], F32, name=f"partner{t}") for t in range(TILES)]
        direct_own = [
            shared.tile([P, H], F32, name=f"direct_own{b}", align_bytes=64, offset=40960 + 2048 * b) for b in range(DIRECT)
        ]
        for t in range(TILES):
            nc.scalar.activation(partner[t][:], h[t][:].indirect(pos_sb[:, 0 : LOW // 16]), COPY)
            if t == 1:
                for b in range(DIRECT):
                    nc.scalar.activation(
                        direct_own[b][:].rearrange("p (u t m) -> p u t m", t=TILES, u=2),
                        in_z_order(banks[6 + b]),
                        COPY,
                        scale=shares[:, 0, b : b + 1],
                    )

        sources = ([h[t][:, LOW:S] for t in range(TILES)], [scaled[t][:] for t in range(TILES)])
        steps = [(0, 2), (0, 3), (0, 0), (0, 1), (1, 0), (1, 1), (1, 2), (1, 3)]

        def add_turned(g, some):
            for half, t in some:
                for b in (2 * g, 2 * g + 1):
                    nc.tensor.matmul(
                        banks[b][:, t * P : (t + 1) * P],
                        sources[half][t][:, b * P : (b + 1) * P],
                        ident[:],
                        start=(half, t) == steps[0],
                        stop=(half, t) == steps[-1],
                        is_transpose=True,
                    )

        for some in (steps[0:5], steps[5:6]):
            for g in range(PAIRS):
                add_turned(g, some)
        add_turned(0, steps[6:])
        add_turned(1, steps[6:])
        for b in range(DIRECT):
            for t in range(TILES):
                nc.tensor.transpose(
                    banks[6 + b][:].rearrange("p (u t m) -> p t u m", t=TILES, u=2)[:, t],
                    partner[t][:, b * P : (b + 1) * P],
                    ident[:],
                )
        add_turned(2, steps[6:])

        z_t = [keep.tile([P, H], BF16, name=f"z_t{b}") for b in range(BLOCKS)]
        for b in range(SUMMED):
            nc.scalar.activation(
                z_t[DIRECT + b][:].rearrange("p (u t m) -> p u t m", t=TILES, u=2),
                in_z_order(banks[b]),
                COPY,
                scale=pivot[:, b : b + 1],
            )
        for b in range(DIRECT):
            nc.vector.scalar_tensor_tensor(
                z_t[b][:], banks[6 + b][:], shares[:, 1, b : b + 1], direct_own[b][:], MULT, ADD
            )

        w2_code = shared.tile([P, N], U32, name="w2_code", align_bytes=64, offset=40960)
        w2_scale = keep.tile([P, N], U8, name="w2_scale", align_bytes=64)
        nc.vector.quantize_mx(w2_code[:].bitcast(FP8X4), w2_scale[:], w2_grouped[:])

        z = {}

        def turn_back(b0, nb, bank, copy):
            pairs = banks[bank][:, 0 : nb * 2 * P].rearrange("p (i u n) -> p i u n", i=nb, u=2)
            for i in range(nb):
                for u in range(2):
                    nc.tensor.transpose(
                        pairs[:, i, u, :], z_t[b0 + i][:].bitcast(F32)[:, u * P : (u + 1) * P], ident[:]
                    )
            z[b0] = shared.tile([P, 4 * nb * P], BF16, name=f"z{b0}", align_bytes=64, offset=28672 + 1024 * b0)
            copy(
                z[b0][:].bitcast(F32).rearrange("p (i c j u) -> p i c u j", i=nb, j=2, u=2),
                pairs.rearrange("p i u (c j) -> p i c u j", j=2),
            )

        def second_layer(b0, nb, bank):
            n = nb * P
            z_code = keep.tile([P, n], U32, name=f"z_code{b0}", align_bytes=64)
            z_scale = keep.tile([P, n], U8, name=f"z_scale{b0}", align_bytes=64)
            nc.vector.quantize_mx(z_code[:].bitcast(FP8X4), z_scale[:], z[b0][:])
            nc.tensor.matmul_mx(
                banks[bank][:, 0:n],
                lhsT=w2_code[:].bitcast(FP8X4),
                lhsT_scale=w2_scale[:],
                rhs=z_code[:].bitcast(FP8X4),
                rhs_scale=z_scale[:],
                start=True,
                stop=True,
            )

        def store(b0, nb, bank, copy, offset):
            n = nb * P
            res = shared.tile([P, n], F32, name=f"res{b0}", align_bytes=64, offset=offset)
            copy(res[:], banks[bank][:, 0:n])
            nc.sync.dma_start(out[:, b0 * P : b0 * P + n], res[:])

        turn_back(2, 2, 0, nc.vector.tensor_copy)
        turn_back(0, 2, 1, nc.vector.tensor_copy)
        turn_back(4, 2, 2, nc.scalar.copy)
        turn_back(6, 1, 4, nc.scalar.copy)
        turn_back(7, 1, 3, nc.scalar.copy)
        groups = [(2, 2, 6), (0, 2, 7), (4, 2, 0), (6, 1, 5), (7, 1, 1)]
        for group in groups:
            second_layer(*group)
        store(*groups[0], nc.scalar.copy, 36864)
        store(*groups[1], nc.scalar.copy, 37888)
        store(*groups[2], nc.vector.tensor_copy, 35840)
        store(*groups[3], nc.scalar.copy, 38912)
        store(*groups[4], nc.scalar.copy, 39936)
